import numpy as np
import ml_dtypes


def mxq(x, axis, fmt="e4m3"):
    dtype, down = {"e4m3": (ml_dtypes.float8_e4m3fn, 7), "e5m2": (ml_dtypes.float8_e5m2, 14)}[fmt]
    v = np.moveaxis(np.asarray(x, np.float32).astype(ml_dtypes.bfloat16).astype(np.float64), axis, -1)
    blocks = v.reshape(v.shape[:-1] + (-1, 32))
    amax = np.abs(blocks).max(-1, keepdims=True)
    byte = np.maximum(np.where(amax > 0, np.frexp(amax)[1] - 1 + 127, 0) - down, 1)
    scale = np.exp2(byte - 127.0)
    codes = (blocks / scale).astype(np.float32).astype(dtype).astype(np.float64)
    return np.moveaxis((codes * scale).reshape(v.shape), -1, axis)


WIDE = False


def mx_kscale(k):
    if not WIDE:
        return np.ones(k)
    levels = np.array([10, -10, 5, -5, 0])
    if k % 512:
        return np.exp2(np.random.permutation(np.resize(levels, k // 32))).repeat(32)
    a = np.empty((k // 512, 16))
    for p in range(k // 512):
        a[p, :8] = np.random.permutation(np.resize(levels, 8))
        for g in range(8):
            far = levels[np.abs(levels - a[p, g]) >= 10]
            a[p, g + 8] = far[np.random.randint(len(far))]
    return np.exp2(a.ravel()).repeat(32)


def f64(x):
    return np.asarray(x).astype(np.float64)


def striped(idx):
    return np.tile(idx.reshape(-1, 16).T, (8, 1)).astype(np.uint16)


def unstriped(offs):
    return offs[:16].T.reshape(-1).astype(np.int64)


E2M1 = np.array([0.0, 0.5, 1.0, 1.5, 2.0, 3.0, 4.0, 6.0, -0.0, -0.5, -1.0, -1.5, -2.0, -3.0, -4.0, -6.0])


def pack_weight(w, fmt):
    k, n = w.shape
    w = f64(np.asarray(w, np.float32).astype(ml_dtypes.bfloat16)).reshape(k // 32, 32, n)
    amax = np.abs(w).max(1)
    if fmt == "e4m3":
        byte = np.frexp(amax)[1] - 1 + 127 - 7
    else:
        mant, ex = np.frexp(amax / 6.0)
        byte = np.where(mant > 0.5, ex, ex - 1) + 127
    byte = np.clip(np.where(amax > 0, byte, 1), 1, 254)
    scaled = (w * np.exp2(127.0 - byte)[:, None, :]).reshape(k, n).astype(np.float32)
    by_word = np.ascontiguousarray(scaled.reshape(k // 512, 128, 4, n).transpose(0, 1, 3, 2))
    if fmt == "e4m3":
        words = by_word.astype(ml_dtypes.float8_e4m3fn).view(np.uint8)
    else:
        c = by_word.astype(ml_dtypes.float4_e2m1fn).view(np.uint8) & 0xF
        words = (c[..., 0::2] | (c[..., 1::2] << 4)).reshape(k // 512, 128, 2 * n)
    return np.ascontiguousarray(words), np.ascontiguousarray(byte.astype(np.uint8).reshape(k // 512, 16, n))


def unpack_weight(words, scales, fmt):
    g, _, n = scales.shape
    words = np.ascontiguousarray(words).reshape(g, 128, n, -1)
    if fmt == "e4m3":
        vals = words.view(ml_dtypes.float8_e4m3fn).astype(np.float64)
    else:
        nib = np.empty((g, 128, n, 4), np.uint8)
        nib[..., 0::2] = words & 0xF
        nib[..., 1::2] = words >> 4
        vals = E2M1[nib]
    vals = vals * np.repeat(np.exp2(scales.astype(np.float64) - 127.0), 8, axis=1)[..., None]
    return vals.transpose(0, 1, 3, 2).reshape(g * 512, n)


def gelu(v):
    return 0.5 * v * (1.0 + np.tanh(np.sqrt(2.0 / np.pi) * (v + 0.044715 * v**3)))


K, T, S, S2 = 1024, 2048, 512, 1024


def setup_inputs():
    n = np.random.standard_normal
    s = mx_kscale(K)[:, None]
    d = {}
    d["tab_words"], d["tab_scales"] = pack_weight(n((K, T)) * s, "e4m3")
    d["offs"] = striped(np.random.permutation(T)[:S])
    d["offs2"] = striped(np.random.permutation(T)[:S2])
    d["wa"] = (n((K, K)) / K**0.5 / s).astype(np.float32)
    d["wb_words"], d["wb_scales"] = pack_weight(n((K, K)) / K**0.5 / s, "e2m1")
    d["gain"] = (1.5 * np.exp(0.3 * n(K)) / K**0.5 / s[:, 0]).astype(np.float32)
    d["level"] = (0.5 * n(S2)).astype(np.float32)
    return d


def reference(tab_words, tab_scales, offs, offs2, wa, wb_words, wb_scales, gain, level):
    TW = unpack_weight(tab_words, tab_scales, "e4m3")
    v = TW[:, unstriped(offs)]
    v2 = TW[:, unstriped(offs2)]
    wb = unpack_weight(wb_words, wb_scales, "e2m1")
    a = mxq(f64(wa), 0, "e4m3").T @ v
    b = wb.T @ v
    h = a * b * f64(gain)[:, None]
    e = v2.T @ mxq(h, 0, "e4m3")
    return np.sqrt(1.0 + np.square(e)) - f64(level)[:, None]

@@ -1,0 +1,234 @@
+from contextlib import ExitStack
+
+import concourse.mybir as mybir
+
+F32 = mybir.dt.float32
+BF16 = mybir.dt.bfloat16
+I32 = mybir.dt.int32
+U32 = mybir.dt.uint32
+U16 = mybir.dt.uint16
+U8 = mybir.dt.uint8
+FP8X4 = mybir.dt.float8_e4m3fn_x4
+FP4X4 = mybir.dt.float4_e2m1fn_x4
+ACT = mybir.ActivationFunctionType
+ALU = mybir.AluOpType
+
+K, T, S, S2 = 1024, 2048, 512, 1024
+P = 128
+PASS = 512
+FLOPS = 2 * K * K * S * 2 + 2 * K * S2 * S
+
+
+def tile_list_bond_strength_screen_kernel(tc, tab_words, tab_scales, offs, offs2, wa, wb_words, wb_scales, gain, level, out):
+    nc = tc.nc
+    with ExitStack() as ctx:
+        keep = ctx.enter_context(tc.tile_pool(name="keep", bufs=1))
+        staged = ctx.enter_context(tc.tile_pool(name="staged", bufs=1))
+        ring = ctx.enter_context(tc.tile_pool(name="ring", bufs=3))
+        psum = ctx.enter_context(tc.psum_pool(name="psum", bufs=1))
+
+        places = {"wb_w_raw": 6144, "gain_sb": 8192,
+                  "wa_raw000": 10240, "tab_w1": 12288,
+                  "wa_raw00256": 20480, "wa_raw010": 22528,
+                  "wa_raw110": 30720, "wa_bf00": 32768, "wa_raw11256": 34816,
+                  "wa_bf11": 40960, "v2_w00": 40960, "v2_w10": 41984,
+                  "h_bf10": 45056, "v2_w01": 45056, "v2_w11": 46080,
+                  "v2_w02": 47104, "h_bf11": 48640, "v2_s1": 49152, "v2_w12": 49664}
+
+        def held(shape, dtype, name, tag=None):
+            if name in places:
+                return staged.tile(shape, dtype, name=name, tag=name, align_bytes=64, offset=places[name])
+            return keep.tile(shape, dtype, name=name, tag=tag or name, align_bytes=64)
+
+        idx = keep.tile([P, S // 16], U16, name="idx")
+        idx2 = keep.tile([P, S2 // 16], U16, name="idx2")
+        tab_s = held([P, T], U8, "tab_s")
+        wb_s_raw = held([P, 2 * K], U8, "wb_s_raw", "slot_wa01")
+        v_s1 = held([P, S], U8, "v_s1")
+        warm_in = held([P, 1], F32, "warm_in", "slot_wa00")
+        warm_out = held([P, 1], F32, "warm_out", "slot_tab1")
+        nc.vector.memset(tab_s[:].bitcast(I32), 0)
+        nc.vector.memset(warm_in[:], 1.0)
+        nc.gpsimd.memset(wb_s_raw[:].bitcast(I32), 0)
+        nc.gpsimd.memset(v_s1[:].bitcast(I32), 0)
+
+        tab_w = {}
+
+        def load_tab(a, tag):
+            tab_w[a] = held([P, T], I32, f"tab_w{a}", tag)
+            nc.sync.dma_start(tab_w[a][:], tab_words[a].rearrange("p t i -> p (t i)").bitcast(I32))
+
+        nc.sync.dma_start(idx[:], offs)
+        wb_w_raw = held([P, 2 * 2 * K], U8, "wb_w_raw", "slot_wa10")
+        nc.sync.dma_start(wb_w_raw[:].bitcast(I32).rearrange("p (a n) -> p a n", a=2),
+                          wb_words.bitcast(I32).rearrange("a p n -> p a n"))
+        nc.sync.dma_start(idx2[:], offs2)
+        load_tab(0, None)
+        for q in range(4):
+            nc.scalar.dma_start(tab_s[32 * q : 32 * q + 8, :].bitcast(I32), tab_scales[:, 4 * q : 4 * q + 4, :].bitcast(I32))
+        nc.scalar.activation(warm_out[:], warm_in[:], ACT.Sqrt)
+        for q in range(4):
+            nc.scalar.dma_start(wb_s_raw[32 * q : 32 * q + 4, :].bitcast(I32).rearrange("p (a n) -> p a n", a=2),
+                                wb_scales[:, 4 * q : 4 * q + 4, :].bitcast(I32).rearrange("a q n -> q a n"))
+
+        wa_raw = {}
+
+        def load_wa(a, b, c0, width, tag):
+            raw = held([P, 4, width], F32, f"wa_raw{a}{b}{c0}", tag)
+            rows = wa[PASS * a : PASS * (a + 1), PASS * b + c0 : PASS * b + c0 + width]
+            nc.sync.dma_start(raw[:], rows.rearrange("(p j) c -> p j c", j=4))
+            wa_raw[(a, b, c0)] = raw
+
+        load_wa(0, 0, 0, 256, None)
+        load_wa(0, 0, 256, 256, None)
+        load_wa(1, 0, 0, 512, None)
+
+        v_s = held([P, S], U8, "v_s")
+        nc.vector.tensor_copy(v_s[:], tab_s[:].indirect(idx[:]))
+        nc.sync.dma_start(v_s1[0:100, :].bitcast(I32), v_s[4:104, :].bitcast(I32))
+        wb_w = [held([P, 2 * 2 * PASS], U8, f"wb_w{b}") for b in range(2)]
+        wb_s = [held([P, 2 * PASS], U8, f"wb_s{b}") for b in range(2)]
+
+        def deal_wb_words(b):
+            src = wb_w_raw[:].bitcast(U16).rearrange("p (a b m t) -> p b a t m", a=2, b=2, t=4)
+            nc.vector.tensor_copy(wb_w[b][:].bitcast(U16).rearrange("p (a t m) -> p a t m", a=2, t=4), src[:, b])
+
+        def deal_wb_scales(b):
+            src = wb_s_raw[:].rearrange("p (a b m t) -> p b a t m", a=2, b=2, t=4)
+            nc.vector.tensor_copy(wb_s[b][:].rearrange("p (a t m) -> p a t m", a=2, t=4), src[:, b])
+
+        v_w = [held([P, S], U32, f"v_w{a}") for a in range(2)]
+
+        def gather_v(a):
+            nc.vector.tensor_copy(v_w[a][:], tab_w[a][:].bitcast(U32).indirect(idx[:]))
+
+        b_sb = [held([P, 4, S], F32, f"b_sb{b}") for b in range(2)]
+
+        def product_b(b):
+            for t in range(4):
+                acc = psum.tile([P, S], F32, name="acc_b", tag="acc_b", bufs=2)
+                for a in range(2):
+                    col = PASS * a + P * t
+                    nc.tensor.matmul_mx(acc[:], lhsT=wb_w[b][:, 2 * col : 2 * col + 2 * P].bitcast(FP4X4),
+                                        lhsT_scale=wb_s[b][:, col : col + P],
+                                        rhs=v_w[a][:].bitcast(FP8X4), rhs_scale=(v_s, v_s1)[a][:],
+                                        start=(a == 0), stop=(a == 1))
+                nc.scalar.activation(b_sb[b][:, t, :], acc[:], ACT.Copy, scale=gain_sb[:, b, t : t + 1])
+
+        wa_bf = {}
+        wa_w = {}
+        wa_s = {}
+
+        def round_wa(a, b, c0, width, copy):
+            if (a, b) not in wa_bf:
+                wa_bf[(a, b)] = held([P, 4 * PASS], BF16, f"wa_bf{a}{b}")
+            dst = wa_bf[(a, b)][:].rearrange("p (u e m j) -> p m u j e", u=2, e=2, j=4)
+            copy(dst[:, c0 // 4 : (c0 + width) // 4], wa_raw[(a, b, c0)][:].rearrange("p j (m u e) -> p m u j e", u=2, e=2))
+
+        def quantize_wa(a, b):
+            wa_w[(a, b)] = held([P, PASS], U32, f"wa_w{a}{b}")
+            wa_s[(a, b)] = held([P, PASS], U8, f"wa_s{a}{b}")
+            nc.vector.quantize_mx(wa_w[(a, b)][:].bitcast(FP8X4), wa_s[(a, b)][:], wa_bf[(a, b)][:])
+
+        h_w = {}
+        h_s = {}
+
+        def make_h(b, half):
+            h_bf = held([P, 4 * 256], BF16, f"h_bf{b}{half}")
+            for quarter in range(2):
+                j0 = 256 * half + P * quarter
+                acc = psum.tile([P, 4, P], F32, name="acc_a", tag="acc_a", bufs=3)
+                for t in range(4):
+                    for a in range(2):
+                        nc.tensor.matmul_mx(acc[:, t, :], lhsT=wa_w[(a, b)][:, P * t : P * (t + 1)].bitcast(FP8X4),
+                                            lhsT_scale=wa_s[(a, b)][:, P * t : P * (t + 1)],
+                                            rhs=v_w[a][:, j0 : j0 + P].bitcast(FP8X4), rhs_scale=v_s[4 * a :, j0 : j0 + P],
+                                            start=(a == 0), stop=(a == 1))
+                nc.vector.tensor_tensor(h_bf[:, 4 * P * quarter : 4 * P * (quarter + 1)].rearrange("p (c i t) -> p c t i", i=2, t=4),
+                                        acc[:].rearrange("p t (c i) -> p c t i", i=2),
+                                        b_sb[b][:, :, j0 : j0 + P].rearrange("p t (c i) -> p c t i", i=2), ALU.mult)
+            h_w[(b, half)] = held([P, 256], U32, f"h_w{b}{half}")
+            h_s[(b, half)] = held([P, 256], U8, f"h_s{b}{half}")
+            nc.vector.quantize_mx(h_w[(b, half)][:].bitcast(FP8X4), h_s[(b, half)][:], h_bf[:])
+
+        v2_w = {}
+        v2_s = {}
+
+        def gather_v2_scales(part):
+            v2_s[part] = held([P, 512], U8, f"v2_s{part}")
+            nc.vector.tensor_copy(v2_s[part][:], tab_s[:].indirect(idx2[:, 32 * part : 32 * (part + 1)]))
+
+        def gather_v2_words(pair):
+            for b in range(2):
+                if pair < 2:
+                    v2_w[(b, pair)] = held([P, 256], U32, f"v2_w{b}{pair}")[:]
+                elif pair == 2:
+                    both = held([P, 512], U32, f"v2_w{b}2")
+                    v2_w[(b, 2)] = both[:, 0:256]
+                    v2_w[(b, 3)] = both[:, 256:512]
+                nc.vector.tensor_copy(v2_w[(b, pair)], tab_w[b][:].bitcast(U32).indirect(idx2[:, 16 * pair : 16 * (pair + 1)]))
+
+        def score(half, pair):
+            acc = psum.tile([P, 2, 256], F32, name="acc_e", tag="acc_e", bufs=3)
+            part, c0 = divmod(256 * pair, 512)
+            for i in range(2):
+                cols = slice(c0 + P * i, c0 + P * (i + 1))
+                for b in range(2):
+                    nc.tensor.matmul_mx(acc[:, i, :], lhsT=v2_w[(b, pair)][:, P * i : P * (i + 1)].bitcast(FP8X4), lhsT_scale=v2_s[part][4 * b :, cols],
+                                        rhs=h_w[(b, half)][:].bitcast(FP8X4), rhs_scale=h_s[(b, half)][:],
+                                        start=(b == 0), stop=(b == 1))
+            sq = ring.tile([P, 2, 256], F32, name="sq")
+            nc.scalar.activation(sq[:], acc[:], ACT.Square)
+            root = ring.tile([P, 2, 256], F32, name="root")
+            nc.scalar.activation(root[:], sq[:], ACT.Sqrt, bias=1.0)
+            res = ring.tile([P, 2, 256], F32, name="res", bufs=4)
+            for i in range(2):
+                nc.gpsimd.tensor_scalar(res[:, i, :], root[:, i, :], 1.0, minus_level[:, 2 * pair + i : 2 * pair + i + 1], ALU.mult, ALU.add)
+            rows = out[256 * pair : 256 * (pair + 1), 256 * half : 256 * (half + 1)]
+            nc.sync.dma_start(rows.rearrange("(i p) j -> p i j", p=P), res[:])
+
+        deal_wb_words(0)
+        deal_wb_words(1)
+        gain_sb = held([P, 2, 4], F32, "gain_sb")
+        nc.sync.dma_start(gain_sb[:], gain.rearrange("(b p t) -> p b t", b=2, t=4))
+        gather_v(0)
+        round_wa(0, 0, 0, 256, nc.scalar.copy)
+        load_tab(1, None)
+        round_wa(0, 0, 256, 256, nc.scalar.copy)
+        load_wa(0, 1, 0, 512, None)
+        gather_v(1)
+        deal_wb_scales(0)
+        deal_wb_scales(1)
+        quantize_wa(0, 0)
+        load_wa(1, 1, 0, 256, None)
+        load_wa(1, 1, 256, 256, None)
+        round_wa(1, 0, 0, 512, nc.scalar.copy)
+        quantize_wa(1, 0)
+        level_sb = held([P, S2 // P], F32, "level_sb", "wa_bf10")
+        with nc.allow_non_contiguous_dma(reason="one level a partition"):
+            nc.sync.dma_start(level_sb[:], level.rearrange("(c p) -> p c", p=P))
+        minus_level = held([P, S2 // P], F32, "minus_level")
+        nc.gpsimd.tensor_scalar(minus_level[:], level_sb[:], -1.0, 0.0, ALU.mult, ALU.add)
+        product_b(0)
+        round_wa(0, 1, 0, 512, nc.vector.tensor_copy)
+        quantize_wa(0, 1)
+        round_wa(1, 1, 0, 256, nc.scalar.copy)
+        round_wa(1, 1, 256, 256, nc.vector.tensor_copy)
+        quantize_wa(1, 1)
+        product_b(1)
+        make_h(0, 0)
+        make_h(1, 0)
+        gather_v2_scales(0)
+        gather_v2_words(0)
+        score(0, 0)
+        gather_v2_words(1)
+        score(0, 1)
+        make_h(0, 1)
+        make_h(1, 1)
+        score(1, 0)
+        score(1, 1)
+        gather_v2_scales(1)
+        for pair in range(2, 4):
+            gather_v2_words(pair)
+            score(0, pair)
+            score(1, pair)

@@ -16,219 +16,222 @@ ALU = mybir.AluOpType
 K, T, S, S2 = 1024, 2048, 512, 1024
 P = 128
 PASS = 512
+HALF = 256
 FLOPS = 2 * K * K * S * 2 + 2 * K * S2 * S
+
+HANDOVERS = [
+    ("warm", [("wa_raw00", 8192), ("tab_w1", 8192), ("gain_sb", 64), ("wa_raw10", 8192)]),
+    ("wb_s_raw", [("wa_raw01", 8192), ("wa_raw11", 8192), ("v_w0", 2048), ("v2_s0", 512), ("v_w1", 2048), ("wa_w00", 2048), ("wa_bf00", 4096)]),
+    ("wb_w0", [("wa_bf10", 4096), ("wa_bf01", 4096)]),
+    ("wa_bf11", [("h_bf00", 4096)]),
+    ("h_bf10", [("h_bf01", 2048)]),
+    ("h_bf11", [("v2_s1", 512), ("v2_w01", 2048), ("v2_w11", 2048)]),
+]
+TAKEOVERS = {"v2_w00": "wa_bf00", "v2_w10": "wa_bf00+", "b_sb1": "wa_raw01", "wa_w01": "wa_raw11", "level_sb": "wa_bf10"}
 
 
 def tile_list_bond_strength_screen_kernel(tc, tab_words, tab_scales, offs, offs2, wa, wb_words, wb_scales, gain, level, out):
     nc = tc.nc
+    offset_of = {}
+    span_of = {}
+    end = 0
+    for first, later in HANDOVERS:
+        offset_of[first] = end
+        span_of[first] = sum(size for name, size in later)
+        for name, size in later:
+            offset_of[name] = end
+            end = end + size
+    for name, former in TAKEOVERS.items():
+        offset_of[name] = offset_of[former.replace("+", "")] + (2048 if "+" in former else 0)
+
     with ExitStack() as ctx:
         keep = ctx.enter_context(tc.tile_pool(name="keep", bufs=1))
-        staged = ctx.enter_context(tc.tile_pool(name="staged", bufs=1))
+        shared = ctx.enter_context(tc.tile_pool(name="shared", bufs=1))
         ring = ctx.enter_context(tc.tile_pool(name="ring", bufs=3))
         psum = ctx.enter_context(tc.psum_pool(name="psum", bufs=1))
 
-        places = {"wb_w_raw": 6144, "gain_sb": 8192,
-                  "wa_raw000": 10240, "tab_w1": 12288,
-                  "wa_raw00256": 20480, "wa_raw010": 22528,
-                  "wa_raw110": 30720, "wa_bf00": 32768, "wa_raw11256": 34816,
-                  "wa_bf11": 40960, "v2_w00": 40960, "v2_w10": 41984,
-                  "h_bf10": 45056, "v2_w01": 45056, "v2_w11": 46080,
-                  "v2_w02": 47104, "h_bf11": 48640, "v2_s1": 49152, "v2_w12": 49664}
-
-        def held(shape, dtype, name, tag=None):
-            if name in places:
-                return staged.tile(shape, dtype, name=name, tag=name, align_bytes=64, offset=places[name])
-            return keep.tile(shape, dtype, name=name, tag=tag or name, align_bytes=64)
+        def held(columns, dtype, name, itemsize=1):
+            if name not in offset_of:
+                return keep.tile([P, columns], dtype, name=name, align_bytes=64)[:]
+            wide = span_of.get(name, 0) // itemsize
+            whole = shared.tile([P, max(columns, wide)], dtype, name=name, align_bytes=64, offset=offset_of[name])
+            return whole[:, 0:columns]
 
         idx = keep.tile([P, S // 16], U16, name="idx")
         idx2 = keep.tile([P, S2 // 16], U16, name="idx2")
-        tab_s = held([P, T], U8, "tab_s")
-        wb_s_raw = held([P, 2 * K], U8, "wb_s_raw", "slot_wa01")
-        v_s1 = held([P, S], U8, "v_s1")
-        warm_in = held([P, 1], F32, "warm_in", "slot_wa00")
-        warm_out = held([P, 1], F32, "warm_out", "slot_tab1")
-        nc.vector.memset(tab_s[:].bitcast(I32), 0)
-        nc.vector.memset(warm_in[:], 1.0)
-        nc.gpsimd.memset(wb_s_raw[:].bitcast(I32), 0)
-        nc.gpsimd.memset(v_s1[:].bitcast(I32), 0)
+        tab_s = held(T, U8, "tab_s")
+        wb_s_raw = held(K, U8, "wb_s_raw")
+        wb_s1 = held(K, U8, "wb_s1")
+        v_s1 = held(S, U8, "v_s1")
+        warm = held(2, F32, "warm", 4)
+        nc.vector.memset(tab_s.bitcast(I32), 0)
+        nc.vector.memset(warm[:, 0:1], 1.0)
+        nc.gpsimd.memset(wb_s_raw.bitcast(I32), 0)
+        nc.vector.memset(v_s1.bitcast(I32), 0)
+        nc.vector.memset(wb_s1.bitcast(I32), 0)
 
         tab_w = {}
 
-        def load_tab(a, tag):
-            tab_w[a] = held([P, T], I32, f"tab_w{a}", tag)
-            nc.sync.dma_start(tab_w[a][:], tab_words[a].rearrange("p t i -> p (t i)").bitcast(I32))
-
-        nc.sync.dma_start(idx[:], offs)
-        wb_w_raw = held([P, 2 * 2 * K], U8, "wb_w_raw", "slot_wa10")
-        nc.sync.dma_start(wb_w_raw[:].bitcast(I32).rearrange("p (a n) -> p a n", a=2),
-                          wb_words.bitcast(I32).rearrange("a p n -> p a n"))
-        nc.sync.dma_start(idx2[:], offs2)
-        load_tab(0, None)
-        for q in range(4):
-            nc.scalar.dma_start(tab_s[32 * q : 32 * q + 8, :].bitcast(I32), tab_scales[:, 4 * q : 4 * q + 4, :].bitcast(I32))
-        nc.scalar.activation(warm_out[:], warm_in[:], ACT.Sqrt)
-        for q in range(4):
-            nc.scalar.dma_start(wb_s_raw[32 * q : 32 * q + 4, :].bitcast(I32).rearrange("p (a n) -> p a n", a=2),
-                                wb_scales[:, 4 * q : 4 * q + 4, :].bitcast(I32).rearrange("a q n -> q a n"))
+        def load_tab(a):
+            tab_w[a] = held(T, I32, f"tab_w{a}")
+            nc.sync.dma_start(tab_w[a], tab_words[a].rearrange("p t i -> p (t i)").bitcast(I32))
 
         wa_raw = {}
 
-        def load_wa(a, b, c0, width, tag):
-            raw = held([P, 4, width], F32, f"wa_raw{a}{b}{c0}", tag)
-            rows = wa[PASS * a : PASS * (a + 1), PASS * b + c0 : PASS * b + c0 + width]
-            nc.sync.dma_start(raw[:], rows.rearrange("(p j) c -> p j c", j=4))
-            wa_raw[(a, b, c0)] = raw
+        def load_wa(a, b, pieces):
+            width = PASS // pieces
+            raw = held(4 * PASS, F32, f"wa_raw{a}{b}").rearrange("p (s j c) -> p s j c", s=pieces, j=4)
+            for piece in range(pieces):
+                c0 = PASS * b + width * piece
+                nc.sync.dma_start(raw[:, piece], wa[PASS * a : PASS * (a + 1), c0 : c0 + width].rearrange("(p j) c -> p j c", j=4))
+            wa_raw[(a, b)] = raw
 
-        load_wa(0, 0, 0, 256, None)
-        load_wa(0, 0, 256, 256, None)
-        load_wa(1, 0, 0, 512, None)
+        nc.sync.dma_start(idx[:], offs)
+        wb_w_raw = held(4 * K, U8, "wb_w_raw")
+        nc.sync.dma_start(wb_w_raw.bitcast(I32).rearrange("p (a n) -> p a n", a=2), wb_words.bitcast(I32).rearrange("a p n -> p a n"))
+        nc.sync.dma_start(idx2[:], offs2)
+        load_tab(0)
+        for q in range(4):
+            nc.scalar.dma_start(tab_s[32 * q : 32 * q + 8, :].bitcast(I32), tab_scales[:, 4 * q : 4 * q + 4, :].bitcast(I32))
+        nc.scalar.activation(warm[:, 1:2], warm[:, 0:1], ACT.Sqrt)
+        for q in range(4):
+            nc.gpsimd.dma_start(wb_s_raw[32 * q : 32 * q + 8, :].bitcast(I32), wb_scales[:, 4 * q : 4 * q + 4, :].bitcast(I32))
+        load_wa(0, 0, 1)
+        load_tab(1)
+        gain_sb = held(8, F32, "gain_sb").rearrange("p (b t) -> p b t", b=2)
+        nc.sync.dma_start(gain_sb, gain.rearrange("(b p t) -> p b t", b=2, t=4))
+        load_wa(1, 0, 1)
 
-        v_s = held([P, S], U8, "v_s")
-        nc.vector.tensor_copy(v_s[:], tab_s[:].indirect(idx[:]))
-        nc.sync.dma_start(v_s1[0:100, :].bitcast(I32), v_s[4:104, :].bitcast(I32))
-        wb_w = [held([P, 2 * 2 * PASS], U8, f"wb_w{b}") for b in range(2)]
-        wb_s = [held([P, 2 * PASS], U8, f"wb_s{b}") for b in range(2)]
+        v_s = held(S, U8, "v_s")
+        nc.vector.tensor_copy(v_s, tab_s.indirect(idx[:]))
+        nc.scalar.dma_start(v_s1[0:100, :].bitcast(I32), v_s[4:104, :].bitcast(I32))
 
-        def deal_wb_words(b):
-            src = wb_w_raw[:].bitcast(U16).rearrange("p (a b m t) -> p b a t m", a=2, b=2, t=4)
-            nc.vector.tensor_copy(wb_w[b][:].bitcast(U16).rearrange("p (a t m) -> p a t m", a=2, t=4), src[:, b])
+        wb_w = {}
+        for b in range(2):
+            wb_w[b] = held(4 * PASS, U8, f"wb_w{b}")
+            src = wb_w_raw.bitcast(U16).rearrange("p (a b m t) -> p b a t m", a=2, b=2, t=4)
+            nc.vector.tensor_copy(wb_w[b].bitcast(U16).rearrange("p (a t m) -> p a t m", a=2, t=4), src[:, b])
+        wb_s = held(K, U8, "wb_s")
+        nc.vector.tensor_copy(wb_s.rearrange("p (b t m) -> p b t m", b=2, t=4), wb_s_raw.rearrange("p (b m t) -> p b t m", b=2, t=4))
+        nc.scalar.dma_start(wb_s1[0:100, :].bitcast(I32), wb_s[4:104, :].bitcast(I32))
+        load_wa(0, 1, 2)
+        load_wa(1, 1, 2)
+        v_w = {}
+        v2_s = {}
 
-        def deal_wb_scales(b):
-            src = wb_s_raw[:].rearrange("p (a b m t) -> p b a t m", a=2, b=2, t=4)
-            nc.vector.tensor_copy(wb_s[b][:].rearrange("p (a t m) -> p a t m", a=2, t=4), src[:, b])
+        def gather_v2_scales(part):
+            v2_s[part] = held(512, U8, f"v2_s{part}")
+            nc.vector.tensor_copy(v2_s[part], tab_s.indirect(idx2[:, 32 * part : 32 * (part + 1)]))
 
-        v_w = [held([P, S], U32, f"v_w{a}") for a in range(2)]
+        def gather_v_words(a):
+            v_w[a] = held(S, U32, f"v_w{a}")
+            nc.vector.tensor_copy(v_w[a], tab_w[a].bitcast(U32).indirect(idx[:]))
 
-        def gather_v(a):
-            nc.vector.tensor_copy(v_w[a][:], tab_w[a][:].bitcast(U32).indirect(idx[:]))
+        gather_v_words(0)
+        gather_v2_scales(0)
+        gather_v_words(1)
 
-        b_sb = [held([P, 4, S], F32, f"b_sb{b}") for b in range(2)]
+        b_sb = {}
 
         def product_b(b):
+            b_sb[b] = held(4 * S, F32, f"b_sb{b}").rearrange("p (t j) -> p t j", t=4)
             for t in range(4):
-                acc = psum.tile([P, S], F32, name="acc_b", tag="acc_b", bufs=2)
+                acc = psum.tile([P, S], F32, name="acc_b", tag="acc_wide", bufs=4)
                 for a in range(2):
                     col = PASS * a + P * t
-                    nc.tensor.matmul_mx(acc[:], lhsT=wb_w[b][:, 2 * col : 2 * col + 2 * P].bitcast(FP4X4),
-                                        lhsT_scale=wb_s[b][:, col : col + P],
-                                        rhs=v_w[a][:].bitcast(FP8X4), rhs_scale=(v_s, v_s1)[a][:],
-                                        start=(a == 0), stop=(a == 1))
+                    nc.tensor.matmul_mx(acc[:], lhsT=wb_w[b][:, 2 * col : 2 * col + 2 * P].bitcast(FP4X4), lhsT_scale=(wb_s, wb_s1)[a][:, PASS * b + P * t : PASS * b + P * (t + 1)],
+                                        rhs=v_w[a].bitcast(FP8X4), rhs_scale=(v_s, v_s1)[a], start=(a == 0), stop=(a == 1))
                 nc.scalar.activation(b_sb[b][:, t, :], acc[:], ACT.Copy, scale=gain_sb[:, b, t : t + 1])
 
         wa_bf = {}
         wa_w = {}
         wa_s = {}
 
-        def round_wa(a, b, c0, width, copy):
-            if (a, b) not in wa_bf:
-                wa_bf[(a, b)] = held([P, 4 * PASS], BF16, f"wa_bf{a}{b}")
-            dst = wa_bf[(a, b)][:].rearrange("p (u e m j) -> p m u j e", u=2, e=2, j=4)
-            copy(dst[:, c0 // 4 : (c0 + width) // 4], wa_raw[(a, b, c0)][:].rearrange("p j (m u e) -> p m u j e", u=2, e=2))
+        def round_wa(a, b, copies):
+            wa_bf[(a, b)] = held(4 * PASS, BF16, f"wa_bf{a}{b}", 2)
+            dst = wa_bf[(a, b)].rearrange("p (u e m j) -> p m u j e", u=2, e=2, j=4)
+            share = P // len(copies)
+            for piece, copy in enumerate(copies):
+                copy(dst[:, share * piece : share * (piece + 1)], wa_raw[(a, b)][:, piece].rearrange("p j (m u e) -> p m u j e", u=2, e=2))
 
         def quantize_wa(a, b):
-            wa_w[(a, b)] = held([P, PASS], U32, f"wa_w{a}{b}")
-            wa_s[(a, b)] = held([P, PASS], U8, f"wa_s{a}{b}")
-            nc.vector.quantize_mx(wa_w[(a, b)][:].bitcast(FP8X4), wa_s[(a, b)][:], wa_bf[(a, b)][:])
+            wa_w[(a, b)] = held(PASS, U32, f"wa_w{a}{b}")
+            wa_s[(a, b)] = held(PASS, U8, f"wa_s{a}{b}")
+            nc.vector.quantize_mx(wa_w[(a, b)].bitcast(FP8X4), wa_s[(a, b)], wa_bf[(a, b)])
 
         h_w = {}
         h_s = {}
 
         def make_h(b, half):
-            h_bf = held([P, 4 * 256], BF16, f"h_bf{b}{half}")
+            h_bf = held(4 * HALF, BF16, f"h_bf{b}{half}", 2)
             for quarter in range(2):
-                j0 = 256 * half + P * quarter
-                acc = psum.tile([P, 4, P], F32, name="acc_a", tag="acc_a", bufs=3)
-                for t in range(4):
-                    for a in range(2):
+                j0 = HALF * half + P * quarter
+                acc = psum.tile([P, 4, P], F32, name="acc_a", tag=f"acc_a{b}", bufs=2)
+                for a in range(2):
+                    for t in range(4):
                         nc.tensor.matmul_mx(acc[:, t, :], lhsT=wa_w[(a, b)][:, P * t : P * (t + 1)].bitcast(FP8X4),
                                             lhsT_scale=wa_s[(a, b)][:, P * t : P * (t + 1)],
                                             rhs=v_w[a][:, j0 : j0 + P].bitcast(FP8X4), rhs_scale=v_s[4 * a :, j0 : j0 + P],
-                                            start=(a == 0), stop=(a == 1))
+                                            start=(a == 0 and t == 0), stop=(a == 1 and t == 3))
                 nc.vector.tensor_tensor(h_bf[:, 4 * P * quarter : 4 * P * (quarter + 1)].rearrange("p (c i t) -> p c t i", i=2, t=4),
                                         acc[:].rearrange("p t (c i) -> p c t i", i=2),
                                         b_sb[b][:, :, j0 : j0 + P].rearrange("p t (c i) -> p c t i", i=2), ALU.mult)
-            h_w[(b, half)] = held([P, 256], U32, f"h_w{b}{half}")
-            h_s[(b, half)] = held([P, 256], U8, f"h_s{b}{half}")
-            nc.vector.quantize_mx(h_w[(b, half)][:].bitcast(FP8X4), h_s[(b, half)][:], h_bf[:])
+            h_w[(b, half)] = held(HALF, U32, f"h_w{b}{half}")
+            h_s[(b, half)] = held(HALF, U8, f"h_s{b}{half}")
+            nc.vector.quantize_mx(h_w[(b, half)].bitcast(FP8X4), h_s[(b, half)], h_bf)
 
         v2_w = {}
-        v2_s = {}
 
-        def gather_v2_scales(part):
-            v2_s[part] = held([P, 512], U8, f"v2_s{part}")
-            nc.vector.tensor_copy(v2_s[part][:], tab_s[:].indirect(idx2[:, 32 * part : 32 * (part + 1)]))
+        def gather_v2_words(b, m0, count):
+            part, c0 = divmod(m0, 512)
+            if c0 == 0:
+                v2_w[(b, part)] = held(512, U32, f"v2_w{b}{part}")
+            nc.vector.tensor_copy(v2_w[(b, part)][:, c0 : c0 + count], tab_w[b].bitcast(U32).indirect(idx2[:, m0 // 16 : (m0 + count) // 16]))
 
-        def gather_v2_words(pair):
-            for b in range(2):
-                if pair < 2:
-                    v2_w[(b, pair)] = held([P, 256], U32, f"v2_w{b}{pair}")[:]
-                elif pair == 2:
-                    both = held([P, 512], U32, f"v2_w{b}2")
-                    v2_w[(b, 2)] = both[:, 0:256]
-                    v2_w[(b, 3)] = both[:, 256:512]
-                nc.vector.tensor_copy(v2_w[(b, pair)], tab_w[b][:].bitcast(U32).indirect(idx2[:, 16 * pair : 16 * (pair + 1)]))
-
-        def score(half, pair):
-            acc = psum.tile([P, 2, 256], F32, name="acc_e", tag="acc_e", bufs=3)
-            part, c0 = divmod(256 * pair, 512)
+        def score(half, pair, engine):
+            acc = psum.tile([P, 2, HALF], F32, name="acc_e", tag="acc_wide", bufs=4)
             for i in range(2):
-                cols = slice(c0 + P * i, c0 + P * (i + 1))
+                m0 = P * (2 * pair + i)
+                part, c0 = divmod(m0, 512)
                 for b in range(2):
-                    nc.tensor.matmul_mx(acc[:, i, :], lhsT=v2_w[(b, pair)][:, P * i : P * (i + 1)].bitcast(FP8X4), lhsT_scale=v2_s[part][4 * b :, cols],
-                                        rhs=h_w[(b, half)][:].bitcast(FP8X4), rhs_scale=h_s[(b, half)][:],
-                                        start=(b == 0), stop=(b == 1))
-            sq = ring.tile([P, 2, 256], F32, name="sq")
+                    nc.tensor.matmul_mx(acc[:, i, :], lhsT=v2_w[(b, part)][:, c0 : c0 + P].bitcast(FP8X4), lhsT_scale=v2_s[part][4 * b :, c0 : c0 + P],
+                                        rhs=h_w[(b, half)].bitcast(FP8X4), rhs_scale=h_s[(b, half)], start=(b == 0), stop=(b == 1))
+            sq = ring.tile([P, 2, HALF], F32, name="sq")
             nc.scalar.activation(sq[:], acc[:], ACT.Square)
-            root = ring.tile([P, 2, 256], F32, name="root")
+            root = ring.tile([P, 2, HALF], F32, name="root", bufs=3)
             nc.scalar.activation(root[:], sq[:], ACT.Sqrt, bias=1.0)
-            res = ring.tile([P, 2, 256], F32, name="res", bufs=4)
+            res = ring.tile([P, 2, HALF], F32, name="res", bufs=4)
             for i in range(2):
-                nc.gpsimd.tensor_scalar(res[:, i, :], root[:, i, :], 1.0, minus_level[:, 2 * pair + i : 2 * pair + i + 1], ALU.mult, ALU.add)
-            rows = out[256 * pair : 256 * (pair + 1), 256 * half : 256 * (half + 1)]
+                engine.tensor_scalar(res[:, i, :], root[:, i, :], level_sb[:, 2 * pair + i : 2 * pair + i + 1], None, ALU.subtract)
+            rows = out[HALF * pair : HALF * (pair + 1), HALF * half : HALF * (half + 1)]
             nc.sync.dma_start(rows.rearrange("(i p) j -> p i j", p=P), res[:])
 
-        deal_wb_words(0)
-        deal_wb_words(1)
-        gain_sb = held([P, 2, 4], F32, "gain_sb")
-        nc.sync.dma_start(gain_sb[:], gain.rearrange("(b p t) -> p b t", b=2, t=4))
-        gather_v(0)
-        round_wa(0, 0, 0, 256, nc.scalar.copy)
-        load_tab(1, None)
-        round_wa(0, 0, 256, 256, nc.scalar.copy)
-        load_wa(0, 1, 0, 512, None)
-        gather_v(1)
-        deal_wb_scales(0)
-        deal_wb_scales(1)
+        round_wa(0, 0, [nc.scalar.copy])
         quantize_wa(0, 0)
-        load_wa(1, 1, 0, 256, None)
-        load_wa(1, 1, 256, 256, None)
-        round_wa(1, 0, 0, 512, nc.scalar.copy)
-        quantize_wa(1, 0)
-        level_sb = held([P, S2 // P], F32, "level_sb", "wa_bf10")
-        with nc.allow_non_contiguous_dma(reason="one level a partition"):
-            nc.sync.dma_start(level_sb[:], level.rearrange("(c p) -> p c", p=P))
-        minus_level = held([P, S2 // P], F32, "minus_level")
-        nc.gpsimd.tensor_scalar(minus_level[:], level_sb[:], -1.0, 0.0, ALU.mult, ALU.add)
+        gather_v2_words(0, 0, 512)
+        gather_v2_words(1, 0, 512)
         product_b(0)
-        round_wa(0, 1, 0, 512, nc.vector.tensor_copy)
-        quantize_wa(0, 1)
-        round_wa(1, 1, 0, 256, nc.scalar.copy)
-        round_wa(1, 1, 256, 256, nc.vector.tensor_copy)
-        quantize_wa(1, 1)
+        round_wa(1, 0, [nc.scalar.copy])
+        round_wa(0, 1, [nc.vector.tensor_copy, nc.scalar.copy])
         product_b(1)
+        round_wa(1, 1, [nc.vector.tensor_copy, nc.vector.tensor_copy])
+        quantize_wa(1, 0)
+        level_sb = held(S2 // P, F32, "level_sb")
+        with nc.allow_non_contiguous_dma(reason="one level a partition"):
+            nc.sync.dma_start(level_sb, level.rearrange("(c p) -> p c", p=P))
+        quantize_wa(1, 1)
+        quantize_wa(0, 1)
         make_h(0, 0)
         make_h(1, 0)
-        gather_v2_scales(0)
-        gather_v2_words(0)
-        score(0, 0)
-        gather_v2_words(1)
-        score(0, 1)
+        score(0, 0, nc.vector)
+        score(0, 1, nc.vector)
         make_h(0, 1)
         make_h(1, 1)
-        score(1, 0)
-        score(1, 1)
+        score(1, 0, nc.vector)
+        score(1, 1, nc.vector)
         gather_v2_scales(1)
-        for pair in range(2, 4):
-            gather_v2_words(pair)
-            score(0, pair)
-            score(1, pair)
+        for pair, engine in ((2, nc.vector), (3, nc.vector)):
+            for b in range(2):
+                gather_v2_words(b, HALF * pair, HALF)
+            score(0, pair, engine)
+            score(1, pair, engine)

@@ -19,15 +19,16 @@ PASS = 512
 HALF = 256
 FLOPS = 2 * K * K * S * 2 + 2 * K * S2 * S
 
+SCORE_BANKS = (2, 3, 0, 1)
 HANDOVERS = [
-    ("warm", [("wa_raw00", 8192), ("tab_w1", 8192), ("gain_sb", 64), ("wa_raw10", 8192)]),
-    ("wb_s_raw", [("wa_raw01", 8192), ("wa_raw11", 8192), ("v_w0", 2048), ("v2_s0", 512), ("v_w1", 2048), ("wa_w00", 2048), ("wa_bf00", 4096)]),
+    ("wb_w_raw", [("warm", 64), ("tab_w1", 8192), ("wa_raw00_0", 8192), ("gain_sb", 64)]),
+    ("wb_s_raw", [("wa_raw10_0", 8192), ("wa_raw01_0", 8192), ("wa_raw11_0", 4096), ("wa_raw11_1", 4096), ("v2_s0", 512), ("wa_w00", 2048)]),
+    ("wa_bf00", [("v2_w00", 2048), ("v2_w10", 2048), ("v2_s1", 512)]),
     ("wb_w0", [("wa_bf10", 4096), ("wa_bf01", 4096)]),
-    ("wa_bf11", [("h_bf00", 4096)]),
-    ("h_bf10", [("h_bf01", 2048)]),
-    ("h_bf11", [("v2_s1", 512), ("v2_w01", 2048), ("v2_w11", 2048)]),
+    ("h_bf10", [("v2_w01", 1024), ("v2_w11", 1024), ("h_bf11", 2048)]),
 ]
-TAKEOVERS = {"v2_w00": "wa_bf00", "v2_w10": "wa_bf00+", "b_sb1": "wa_raw01", "wa_w01": "wa_raw11", "level_sb": "wa_bf10"}
+TAKEOVERS = [("b_sb1", "wa_raw01_0", 0), ("level_sb", "wa_raw10_0", 0), ("v2_w02", "h_bf11", 0), ("v2_w12", "h_bf11", 1024),
+             ("res0", "tab_w1", 0), ("res1", "tab_w1", 2048), ("res2", "tab_w1", 4096), ("res3", "tab_w1", 6144)]
 
 
 def tile_list_bond_strength_screen_kernel(tc, tab_words, tab_scales, offs, offs2, wa, wb_words, wb_scales, gain, level, out):
@@ -41,8 +42,9 @@ def tile_list_bond_strength_screen_kernel(tc, tab_words, tab_scales, offs, offs2
         for name, size in later:
             offset_of[name] = end
             end = end + size
-    for name, former in TAKEOVERS.items():
-        offset_of[name] = offset_of[former.replace("+", "")] + (2048 if "+" in former else 0)
+        end = max(end, offset_of[first] + 4096)
+    for name, former, skip in TAKEOVERS:
+        offset_of[name] = offset_of[former] + skip
 
     with ExitStack() as ctx:
         keep = ctx.enter_context(tc.tile_pool(name="keep", bufs=1))
@@ -63,9 +65,7 @@ def tile_list_bond_strength_screen_kernel(tc, tab_words, tab_scales, offs, offs2
         wb_s_raw = held(K, U8, "wb_s_raw")
         wb_s1 = held(K, U8, "wb_s1")
         v_s1 = held(S, U8, "v_s1")
-        warm = held(2, F32, "warm", 4)
         nc.vector.memset(tab_s.bitcast(I32), 0)
-        nc.vector.memset(warm[:, 0:1], 1.0)
         nc.gpsimd.memset(wb_s_raw.bitcast(I32), 0)
         nc.vector.memset(v_s1.bitcast(I32), 0)
         nc.vector.memset(wb_s1.bitcast(I32), 0)
@@ -80,42 +80,13 @@ def tile_list_bond_strength_screen_kernel(tc, tab_words, tab_scales, offs, offs2
 
         def load_wa(a, b, pieces):
             width = PASS // pieces
-            raw = held(4 * PASS, F32, f"wa_raw{a}{b}").rearrange("p (s j c) -> p s j c", s=pieces, j=4)
             for piece in range(pieces):
+                raw = held(4 * width, F32, f"wa_raw{a}{b}_{piece}").rearrange("p (j c) -> p j c", j=4)
                 c0 = PASS * b + width * piece
-                nc.sync.dma_start(raw[:, piece], wa[PASS * a : PASS * (a + 1), c0 : c0 + width].rearrange("(p j) c -> p j c", j=4))
-            wa_raw[(a, b)] = raw
-
-        nc.sync.dma_start(idx[:], offs)
-        wb_w_raw = held(4 * K, U8, "wb_w_raw")
-        nc.sync.dma_start(wb_w_raw.bitcast(I32).rearrange("p (a n) -> p a n", a=2), wb_words.bitcast(I32).rearrange("a p n -> p a n"))
-        nc.sync.dma_start(idx2[:], offs2)
-        load_tab(0)
-        for q in range(4):
-            nc.scalar.dma_start(tab_s[32 * q : 32 * q + 8, :].bitcast(I32), tab_scales[:, 4 * q : 4 * q + 4, :].bitcast(I32))
-        nc.scalar.activation(warm[:, 1:2], warm[:, 0:1], ACT.Sqrt)
-        for q in range(4):
-            nc.gpsimd.dma_start(wb_s_raw[32 * q : 32 * q + 8, :].bitcast(I32), wb_scales[:, 4 * q : 4 * q + 4, :].bitcast(I32))
-        load_wa(0, 0, 1)
-        load_tab(1)
-        gain_sb = held(8, F32, "gain_sb").rearrange("p (b t) -> p b t", b=2)
-        nc.sync.dma_start(gain_sb, gain.rearrange("(b p t) -> p b t", b=2, t=4))
-        load_wa(1, 0, 1)
-
-        v_s = held(S, U8, "v_s")
-        nc.vector.tensor_copy(v_s, tab_s.indirect(idx[:]))
-        nc.scalar.dma_start(v_s1[0:100, :].bitcast(I32), v_s[4:104, :].bitcast(I32))
+                nc.sync.dma_start(raw, wa[PASS * a : PASS * (a + 1), c0 : c0 + width].rearrange("(p j) c -> p j c", j=4))
+                wa_raw[(a, b, piece)] = raw
 
         wb_w = {}
-        for b in range(2):
-            wb_w[b] = held(4 * PASS, U8, f"wb_w{b}")
-            src = wb_w_raw.bitcast(U16).rearrange("p (a b m t) -> p b a t m", a=2, b=2, t=4)
-            nc.vector.tensor_copy(wb_w[b].bitcast(U16).rearrange("p (a t m) -> p a t m", a=2, t=4), src[:, b])
-        wb_s = held(K, U8, "wb_s")
-        nc.vector.tensor_copy(wb_s.rearrange("p (b t m) -> p b t m", b=2, t=4), wb_s_raw.rearrange("p (b m t) -> p b t m", b=2, t=4))
-        nc.scalar.dma_start(wb_s1[0:100, :].bitcast(I32), wb_s[4:104, :].bitcast(I32))
-        load_wa(0, 1, 2)
-        load_wa(1, 1, 2)
         v_w = {}
         v2_s = {}
 
@@ -127,7 +98,36 @@ def tile_list_bond_strength_screen_kernel(tc, tab_words, tab_scales, offs, offs2
             v_w[a] = held(S, U32, f"v_w{a}")
             nc.vector.tensor_copy(v_w[a], tab_w[a].bitcast(U32).indirect(idx[:]))
 
+        nc.sync.dma_start(idx[:], offs)
+        wb_w_raw = held(4 * K, U8, "wb_w_raw")
+        nc.sync.dma_start(wb_w_raw.bitcast(I32).rearrange("p (a n) -> p a n", a=2), wb_words.bitcast(I32).rearrange("a p n -> p a n"))
+        nc.sync.dma_start(idx2[:], offs2)
+        load_tab(0)
+        for q in range(4):
+            nc.scalar.dma_start(tab_s[32 * q : 32 * q + 8, :].bitcast(I32), tab_scales[:, 4 * q : 4 * q + 4, :].bitcast(I32))
+        for q in range(4):
+            nc.scalar.dma_start(wb_s_raw[32 * q : 32 * q + 8, :].bitcast(I32), wb_scales[:, 4 * q : 4 * q + 4, :].bitcast(I32))
+        for b in range(2):
+            wb_w[b] = held(4 * PASS, U8, f"wb_w{b}")
+            src = wb_w_raw.bitcast(U16).rearrange("p (a b m t) -> p b a t m", a=2, b=2, t=4)
+            nc.vector.tensor_copy(wb_w[b].bitcast(U16).rearrange("p (a t m) -> p a t m", a=2, t=4), src[:, b])
+        load_wa(0, 0, 1)
+        load_tab(1)
+        gain_sb = held(8, F32, "gain_sb").rearrange("p (b t) -> p b t", b=2)
+        nc.sync.dma_start(gain_sb, gain.rearrange("(b p t) -> p b t", b=2, t=4))
+        warm = held(2, F32, "warm")
+        nc.gpsimd.memset(warm[:, 0:1], 1.0)
+        nc.scalar.activation(warm[:, 1:2], warm[:, 0:1], ACT.Sqrt)
         gather_v_words(0)
+        v_s = held(S, U8, "v_s")
+        nc.vector.tensor_copy(v_s, tab_s.indirect(idx[:]))
+        nc.scalar.dma_start(v_s1[0:100, :].bitcast(I32), v_s[4:104, :].bitcast(I32))
+        wb_s = held(K, U8, "wb_s")
+        nc.vector.tensor_copy(wb_s.rearrange("p (b t m) -> p b t m", b=2, t=4), wb_s_raw.rearrange("p (b m t) -> p b t m", b=2, t=4))
+        nc.sync.dma_start(wb_s1[0:100, :].bitcast(I32), wb_s[4:104, :].bitcast(I32))
+        load_wa(1, 0, 1)
+        load_wa(0, 1, 1)
+        load_wa(1, 1, 2)
         gather_v2_scales(0)
         gather_v_words(1)
 
@@ -136,7 +136,7 @@ def tile_list_bond_strength_screen_kernel(tc, tab_words, tab_scales, offs, offs2
         def product_b(b):
             b_sb[b] = held(4 * S, F32, f"b_sb{b}").rearrange("p (t j) -> p t j", t=4)
             for t in range(4):
-                acc = psum.tile([P, S], F32, name="acc_b", tag="acc_wide", bufs=4)
+                acc = psum.tile([P, S], F32, name="acc_b", tag=f"bank{t}")
                 for a in range(2):
                     col = PASS * a + P * t
                     nc.tensor.matmul_mx(acc[:], lhsT=wb_w[b][:, 2 * col : 2 * col + 2 * P].bitcast(FP4X4), lhsT_scale=(wb_s, wb_s1)[a][:, PASS * b + P * t : PASS * b + P * (t + 1)],
@@ -149,10 +149,10 @@ def tile_list_bond_strength_screen_kernel(tc, tab_words, tab_scales, offs, offs2
 
         def round_wa(a, b, copies):
             wa_bf[(a, b)] = held(4 * PASS, BF16, f"wa_bf{a}{b}", 2)
-            dst = wa_bf[(a, b)].rearrange("p (u e m j) -> p m u j e", u=2, e=2, j=4)
+            dst = wa_bf[(a, b)].rearrange("p (t m j) -> p m j t", t=4, j=4)
             share = P // len(copies)
             for piece, copy in enumerate(copies):
-                copy(dst[:, share * piece : share * (piece + 1)], wa_raw[(a, b)][:, piece].rearrange("p j (m u e) -> p m u j e", u=2, e=2))
+                copy(dst[:, share * piece : share * (piece + 1)], wa_raw[(a, b, piece)].rearrange("p j (m t) -> p m j t", t=4))
 
         def quantize_wa(a, b):
             wa_w[(a, b)] = held(PASS, U32, f"wa_w{a}{b}")
@@ -162,17 +162,25 @@ def tile_list_bond_strength_screen_kernel(tc, tab_words, tab_scales, offs, offs2
         h_w = {}
         h_s = {}
 
-        def make_h(b, half):
-            h_bf = held(4 * HALF, BF16, f"h_bf{b}{half}", 2)
+        a_acc = {}
+
+        def product_a(b, half, first_bank):
             for quarter in range(2):
                 j0 = HALF * half + P * quarter
-                acc = psum.tile([P, 4, P], F32, name="acc_a", tag=f"acc_a{b}", bufs=2)
-                for a in range(2):
+                acc = psum.tile([P, 4, P], F32, name="acc_a", tag=f"bank{first_bank + quarter}")
+                a_acc[(b, half, quarter)] = acc
+                for step, a in enumerate((b, 1 - b)):
                     for t in range(4):
                         nc.tensor.matmul_mx(acc[:, t, :], lhsT=wa_w[(a, b)][:, P * t : P * (t + 1)].bitcast(FP8X4),
                                             lhsT_scale=wa_s[(a, b)][:, P * t : P * (t + 1)],
                                             rhs=v_w[a][:, j0 : j0 + P].bitcast(FP8X4), rhs_scale=v_s[4 * a :, j0 : j0 + P],
-                                            start=(a == 0 and t == 0), stop=(a == 1 and t == 3))
+                                            start=(step == 0 and t == 0), stop=(step == 1 and t == 3))
+
+        def make_h(b, half):
+            h_bf = held(4 * HALF, BF16, f"h_bf{b}{half}", 2)
+            for quarter in range(2):
+                j0 = HALF * half + P * quarter
+                acc = a_acc[(b, half, quarter)]
                 nc.vector.tensor_tensor(h_bf[:, 4 * P * quarter : 4 * P * (quarter + 1)].rearrange("p (c i t) -> p c t i", i=2, t=4),
                                         acc[:].rearrange("p t (c i) -> p c t i", i=2),
                                         b_sb[b][:, :, j0 : j0 + P].rearrange("p t (c i) -> p c t i", i=2), ALU.mult)
@@ -182,56 +190,73 @@ def tile_list_bond_strength_screen_kernel(tc, tab_words, tab_scales, offs, offs2
 
         v2_w = {}
 
-        def gather_v2_words(b, m0, count):
-            part, c0 = divmod(m0, 512)
-            if c0 == 0:
-                v2_w[(b, part)] = held(512, U32, f"v2_w{b}{part}")
-            nc.vector.tensor_copy(v2_w[(b, part)][:, c0 : c0 + count], tab_w[b].bitcast(U32).indirect(idx2[:, m0 // 16 : (m0 + count) // 16]))
+        def gather_v2_words(m0, count):
+            for b in range(2):
+                words = held(count, U32, f"v2_w{b}{len(v2_w) // 2}")
+                nc.vector.tensor_copy(words, tab_w[b].bitcast(U32).indirect(idx2[:, m0 // 16 : (m0 + count) // 16]))
+                v2_w[(b, m0)] = words
 
-        def score(half, pair, engine):
-            acc = psum.tile([P, 2, HALF], F32, name="acc_e", tag="acc_wide", bufs=4)
-            for i in range(2):
-                m0 = P * (2 * pair + i)
-                part, c0 = divmod(m0, 512)
-                for b in range(2):
-                    nc.tensor.matmul_mx(acc[:, i, :], lhsT=v2_w[(b, part)][:, c0 : c0 + P].bitcast(FP8X4), lhsT_scale=v2_s[part][4 * b :, c0 : c0 + P],
-                                        rhs=h_w[(b, half)].bitcast(FP8X4), rhs_scale=h_s[(b, half)], start=(b == 0), stop=(b == 1))
+        roots = []
+
+        def score(half, pair):
+            acc = psum.tile([P, 2, HALF], F32, name="acc_e", tag=f"bank{SCORE_BANKS[len(roots) % 4]}")
+            for b in range(2):
+                for i in range(2):
+                    m0 = P * (2 * pair + i)
+                    part, c0 = divmod(m0, 512)
+                    first = max(start for pass_b, start in v2_w if start <= m0)
+                    nc.tensor.matmul_mx(acc[:, i, :], lhsT=v2_w[(b, first)][:, m0 - first : m0 - first + P].bitcast(FP8X4), lhsT_scale=v2_s[part][4 * b :, c0 : c0 + P],
+                                        rhs=h_w[(b, half)].bitcast(FP8X4), rhs_scale=h_s[(b, half)], start=(b == 0 and i == 0), stop=(b == 1 and i == 1))
             sq = ring.tile([P, 2, HALF], F32, name="sq")
-            nc.scalar.activation(sq[:], acc[:], ACT.Square)
-            root = ring.tile([P, 2, HALF], F32, name="root", bufs=3)
+            if len(roots) in (7,):
+                plain = ring.tile([P, 2, HALF], F32, name="plain", bufs=2)
+                nc.vector.tensor_copy(plain[:], acc[:])
+                nc.vector.tensor_tensor(sq[:], acc[:], plain[:], ALU.mult)
+            else:
+                nc.scalar.activation(sq[:], acc[:], ACT.Square)
+            root = ring.tile([P, 2, HALF], F32, name="root", bufs=8)
             nc.scalar.activation(root[:], sq[:], ACT.Sqrt, bias=1.0)
-            res = ring.tile([P, 2, HALF], F32, name="res", bufs=4)
+            roots.append((half, pair, root))
+
+        def finish(n):
+            half, pair, root = roots[n]
+            res = held(2 * HALF, F32, f"res{n}").rearrange("p (i j) -> p i j", i=2)
             for i in range(2):
-                engine.tensor_scalar(res[:, i, :], root[:, i, :], level_sb[:, 2 * pair + i : 2 * pair + i + 1], None, ALU.subtract)
+                nc.vector.tensor_scalar(res[:, i, :], root[:, i, :], level_sb[:, 2 * pair + i : 2 * pair + i + 1], None, ALU.subtract)
             rows = out[HALF * pair : HALF * (pair + 1), HALF * half : HALF * (half + 1)]
-            nc.sync.dma_start(rows.rearrange("(i p) j -> p i j", p=P), res[:])
+            nc.sync.dma_start(rows.rearrange("(i p) j -> p i j", p=P), res)
 
         round_wa(0, 0, [nc.scalar.copy])
         quantize_wa(0, 0)
-        gather_v2_words(0, 0, 512)
-        gather_v2_words(1, 0, 512)
+        gather_v2_words(0, 512)
+        gather_v2_scales(1)
         product_b(0)
         round_wa(1, 0, [nc.scalar.copy])
-        round_wa(0, 1, [nc.vector.tensor_copy, nc.scalar.copy])
-        product_b(1)
-        round_wa(1, 1, [nc.vector.tensor_copy, nc.vector.tensor_copy])
         quantize_wa(1, 0)
         level_sb = held(S2 // P, F32, "level_sb")
         with nc.allow_non_contiguous_dma(reason="one level a partition"):
             nc.sync.dma_start(level_sb, level.rearrange("(c p) -> p c", p=P))
+        round_wa(0, 1, [nc.scalar.copy])
+        product_b(1)
+        round_wa(1, 1, [nc.vector.tensor_copy, nc.vector.tensor_copy])
         quantize_wa(1, 1)
         quantize_wa(0, 1)
+        product_a(0, 0, 4)
+        product_a(0, 1, 6)
+        product_a(1, 0, 0)
         make_h(0, 0)
+        product_a(1, 1, 4)
         make_h(1, 0)
-        score(0, 0, nc.vector)
-        score(0, 1, nc.vector)
         make_h(0, 1)
+        score(0, 0)
+        score(0, 1)
+        gather_v2_words(512, HALF)
+        score(0, 2)
         make_h(1, 1)
-        score(1, 0, nc.vector)
-        score(1, 1, nc.vector)
-        gather_v2_scales(1)
-        for pair, engine in ((2, nc.vector), (3, nc.vector)):
-            for b in range(2):
-                gather_v2_words(b, HALF * pair, HALF)
-            score(0, pair, engine)
-            score(1, pair, engine)
+        for pair in range(3):
+            score(1, pair)
+        gather_v2_words(768, HALF)
+        score(0, 3)
+        score(1, 3)
+        for n in range(8):
+            finish(n)

@@ -21,13 +21,12 @@ FLOPS = 2 * K * K * S * 2 + 2 * K * S2 * S
 
 SCORE_BANKS = (2, 3, 0, 1)
 HANDOVERS = [
-    ("wb_w_raw", [("warm", 64), ("tab_w1", 8192), ("wa_raw00_0", 8192), ("gain_sb", 64)]),
-    ("wb_s_raw", [("wa_raw10_0", 8192), ("wa_raw01_0", 8192), ("wa_raw11_0", 4096), ("wa_raw11_1", 4096), ("v2_s0", 512), ("wa_w00", 2048)]),
-    ("wa_bf00", [("v2_w00", 2048), ("v2_w10", 2048), ("v2_s1", 512)]),
+    ("warm", [("wa_raw00_0", 8192), ("gain_sb", 64), ("tab_w1", 8192), ("wa_raw10_0", 8192), ("wb_s_raw", 64)]),
+    ("wb_s_raw", [("wa_raw01_0", 8192), ("wa_raw11_0", 4096), ("wa_raw11_1", 4096), ("v2_s0", 512), ("v_w1", 2048), ("v2_w00", 2048), ("wa_bf00", 4096)]),
     ("wb_w0", [("wa_bf10", 4096), ("wa_bf01", 4096)]),
     ("h_bf10", [("v2_w01", 1024), ("v2_w11", 1024), ("h_bf11", 2048)]),
 ]
-TAKEOVERS = [("b_sb1", "wa_raw01_0", 0), ("level_sb", "wa_raw10_0", 0), ("v2_w02", "h_bf11", 0), ("v2_w12", "h_bf11", 1024),
+TAKEOVERS = [("wa_w11", "wa_bf10", 64), ("v2_w10", "wa_bf00", 0), ("v2_s1", "wa_bf00", 2048), ("b_sb1", "wa_raw01_0", 0), ("level_sb", "wa_bf10", 0), ("v2_w02", "h_bf11", 0), ("v2_w12", "h_bf11", 1024),
              ("res0", "tab_w1", 0), ("res1", "tab_w1", 2048), ("res2", "tab_w1", 4096), ("res3", "tab_w1", 6144)]
 
 
@@ -37,6 +36,7 @@ def tile_list_bond_strength_screen_kernel(tc, tab_words, tab_scales, offs, offs2
     span_of = {}
     end = 0
     for first, later in HANDOVERS:
+        end = offset_of.get(first, end)
         offset_of[first] = end
         span_of[first] = sum(size for name, size in later)
         for name, size in later:
@@ -62,11 +62,11 @@ def tile_list_bond_strength_screen_kernel(tc, tab_words, tab_scales, offs, offs2
         idx = keep.tile([P, S // 16], U16, name="idx")
         idx2 = keep.tile([P, S2 // 16], U16, name="idx2")
         tab_s = held(T, U8, "tab_s")
-        wb_s_raw = held(K, U8, "wb_s_raw")
         wb_s1 = held(K, U8, "wb_s1")
         v_s1 = held(S, U8, "v_s1")
+        warm = held(2, F32, "warm", 4)
         nc.vector.memset(tab_s.bitcast(I32), 0)
-        nc.gpsimd.memset(wb_s_raw.bitcast(I32), 0)
+        nc.vector.memset(warm[:, 0:1], 1.0)
         nc.vector.memset(v_s1.bitcast(I32), 0)
         nc.vector.memset(wb_s1.bitcast(I32), 0)
 
@@ -99,12 +99,15 @@ def tile_list_bond_strength_screen_kernel(tc, tab_words, tab_scales, offs, offs2
             nc.vector.tensor_copy(v_w[a], tab_w[a].bitcast(U32).indirect(idx[:]))
 
         nc.sync.dma_start(idx[:], offs)
+        nc.sync.dma_start(idx2[:], offs2)
         wb_w_raw = held(4 * K, U8, "wb_w_raw")
         nc.sync.dma_start(wb_w_raw.bitcast(I32).rearrange("p (a n) -> p a n", a=2), wb_words.bitcast(I32).rearrange("a p n -> p a n"))
-        nc.sync.dma_start(idx2[:], offs2)
         load_tab(0)
         for q in range(4):
             nc.scalar.dma_start(tab_s[32 * q : 32 * q + 8, :].bitcast(I32), tab_scales[:, 4 * q : 4 * q + 4, :].bitcast(I32))
+        nc.scalar.activation(warm[:, 1:2], warm[:, 0:1], ACT.Sqrt)
+        wb_s_raw = held(K, U8, "wb_s_raw")
+        nc.gpsimd.memset(wb_s_raw.bitcast(I32), 0)
         for q in range(4):
             nc.scalar.dma_start(wb_s_raw[32 * q : 32 * q + 8, :].bitcast(I32), wb_scales[:, 4 * q : 4 * q + 4, :].bitcast(I32))
         for b in range(2):
@@ -112,20 +115,17 @@ def tile_list_bond_strength_screen_kernel(tc, tab_words, tab_scales, offs, offs2
             src = wb_w_raw.bitcast(U16).rearrange("p (a b m t) -> p b a t m", a=2, b=2, t=4)
             nc.vector.tensor_copy(wb_w[b].bitcast(U16).rearrange("p (a t m) -> p a t m", a=2, t=4), src[:, b])
         load_wa(0, 0, 1)
-        load_tab(1)
         gain_sb = held(8, F32, "gain_sb").rearrange("p (b t) -> p b t", b=2)
         nc.sync.dma_start(gain_sb, gain.rearrange("(b p t) -> p b t", b=2, t=4))
-        warm = held(2, F32, "warm")
-        nc.gpsimd.memset(warm[:, 0:1], 1.0)
-        nc.scalar.activation(warm[:, 1:2], warm[:, 0:1], ACT.Sqrt)
+        load_tab(1)
+        load_wa(1, 0, 1)
         gather_v_words(0)
         v_s = held(S, U8, "v_s")
         nc.vector.tensor_copy(v_s, tab_s.indirect(idx[:]))
         nc.scalar.dma_start(v_s1[0:100, :].bitcast(I32), v_s[4:104, :].bitcast(I32))
         wb_s = held(K, U8, "wb_s")
         nc.vector.tensor_copy(wb_s.rearrange("p (b t m) -> p b t m", b=2, t=4), wb_s_raw.rearrange("p (b m t) -> p b t m", b=2, t=4))
-        nc.sync.dma_start(wb_s1[0:100, :].bitcast(I32), wb_s[4:104, :].bitcast(I32))
-        load_wa(1, 0, 1)
+        nc.scalar.dma_start(wb_s1[0:100, :].bitcast(I32), wb_s[4:104, :].bitcast(I32))
         load_wa(0, 1, 1)
         load_wa(1, 1, 2)
         gather_v2_scales(0)
@@ -151,8 +151,9 @@ def tile_list_bond_strength_screen_kernel(tc, tab_words, tab_scales, offs, offs2
             wa_bf[(a, b)] = held(4 * PASS, BF16, f"wa_bf{a}{b}", 2)
             dst = wa_bf[(a, b)].rearrange("p (t m j) -> p m j t", t=4, j=4)
             share = P // len(copies)
-            for piece, copy in enumerate(copies):
-                copy(dst[:, share * piece : share * (piece + 1)], wa_raw[(a, b, piece)].rearrange("p j (m t) -> p m j t", t=4))
+            for n, copy in enumerate(copies):
+                piece, m0 = (n, 0) if (a, b, n) in wa_raw and (a, b, 1) in wa_raw else (0, share * n)
+                copy(dst[:, share * n : share * (n + 1)], wa_raw[(a, b, piece)].rearrange("p j (m t) -> p m j t", t=4)[:, m0 : m0 + share])
 
         def quantize_wa(a, b):
             wa_w[(a, b)] = held(PASS, U32, f"wa_w{a}{b}")
@@ -236,7 +237,7 @@ def tile_list_bond_strength_screen_kernel(tc, tab_words, tab_scales, offs, offs2
         level_sb = held(S2 // P, F32, "level_sb")
         with nc.allow_non_contiguous_dma(reason="one level a partition"):
             nc.sync.dma_start(level_sb, level.rearrange("(c p) -> p c", p=P))
-        round_wa(0, 1, [nc.scalar.copy])
+        round_wa(0, 1, [nc.vector.tensor_copy, nc.scalar.copy])
         product_b(1)
         round_wa(1, 1, [nc.vector.tensor_copy, nc.vector.tensor_copy])
         quantize_wa(1, 1)

@@ -17,17 +17,33 @@ K, T, S, S2 = 1024, 2048, 512, 1024
 P = 128
 PASS = 512
 HALF = 256
+LIST_ROWS = 16
+SHIFT_ROWS = 100
 FLOPS = 2 * K * K * S * 2 + 2 * K * S2 * S
 
-SCORE_BANKS = (2, 3, 0, 1)
+A_BANKS = {(0, 0): 4, (0, 1): 6, (1, 0): 0, (1, 1): 4}
+E_BANKS = (2, 3, 0, 1)
+
 HANDOVERS = [
-    ("warm", [("wa_raw00_0", 8192), ("gain_sb", 64), ("tab_w1", 8192), ("wa_raw10_0", 8192), ("wb_s_raw", 64)]),
-    ("wb_s_raw", [("wa_raw01_0", 8192), ("wa_raw11_0", 4096), ("wa_raw11_1", 4096), ("v2_s0", 512), ("v_w1", 2048), ("v2_w00", 2048), ("wa_bf00", 4096)]),
+    ("one", [("tab_w0", 8192)]),
+    ("wb_s_raw", [("wa_raw10_0", 8192), ("wa_raw01_0", 8192), ("wa_raw11_0", 4096), ("wa_raw11_1", 4096),
+                  ("v2_s0", 512), ("v2_s1", 512), ("wa_w00", 2048)]),
+    ("wb_w_raw", [("wa_raw00_0", 8192), ("tab_w1", 8192), ("gain_sb", 64)]),
+    ("wa_bf00", [("v2_w0_0", 2048), ("v2_w1_0", 2048), ("v2_w0_512", 1024), ("v2_w1_512", 1024)]),
     ("wb_w0", [("wa_bf10", 4096), ("wa_bf01", 4096)]),
-    ("h_bf10", [("v2_w01", 1024), ("v2_w11", 1024), ("h_bf11", 2048)]),
+    ("wa_bf11", [("h_bf00", 2048), ("h_bf01", 2048)]),
+    ("h_bf10", [("h_bf11", 2048)]),
 ]
-TAKEOVERS = [("wa_w11", "wa_bf10", 64), ("v2_w10", "wa_bf00", 0), ("v2_s1", "wa_bf00", 2048), ("b_sb1", "wa_raw01_0", 0), ("level_sb", "wa_bf10", 0), ("v2_w02", "h_bf11", 0), ("v2_w12", "h_bf11", 1024),
-             ("res0", "tab_w1", 0), ("res1", "tab_w1", 2048), ("res2", "tab_w1", 4096), ("res3", "tab_w1", 6144)]
+REGION_MIN = 4096
+TAKEOVERS = [
+    ("wa_w01", "wa_bf10", 64),
+    ("wa_w11", "wa_bf01", 0),
+    ("b_sb1", "wa_raw01_0", 0),
+    ("level_sb", "wa_bf10", 0),
+    ("v2_w0_768", "h_bf11", 0),
+    ("v2_w1_768", "h_bf11", 1024),
+    ("res0", "tab_w1", 0), ("res1", "tab_w1", 2048), ("res2", "tab_w1", 4096), ("res3", "tab_w1", 6144),
+]
 
 
 def tile_list_bond_strength_screen_kernel(tc, tab_words, tab_scales, offs, offs2, wa, wb_words, wb_scales, gain, level, out):
@@ -35,45 +51,48 @@ def tile_list_bond_strength_screen_kernel(tc, tab_words, tab_scales, offs, offs2
     offset_of = {}
     span_of = {}
     end = 0
-    for first, later in HANDOVERS:
-        end = offset_of.get(first, end)
-        offset_of[first] = end
-        span_of[first] = sum(size for name, size in later)
+    for earlier, later in HANDOVERS:
+        offset_of[earlier] = end
+        span_of[earlier] = sum(size for name, size in later)
         for name, size in later:
             offset_of[name] = end
             end = end + size
-        end = max(end, offset_of[first] + 4096)
-    for name, former, skip in TAKEOVERS:
-        offset_of[name] = offset_of[former] + skip
+        end = max(end, offset_of[earlier] + REGION_MIN)
+    for name, earlier, skip in TAKEOVERS:
+        offset_of[name] = offset_of[earlier] + skip
 
     with ExitStack() as ctx:
         keep = ctx.enter_context(tc.tile_pool(name="keep", bufs=1))
         shared = ctx.enter_context(tc.tile_pool(name="shared", bufs=1))
-        ring = ctx.enter_context(tc.tile_pool(name="ring", bufs=3))
+        ring = ctx.enter_context(tc.tile_pool(name="ring", bufs=1))
         psum = ctx.enter_context(tc.psum_pool(name="psum", bufs=1))
 
-        def held(columns, dtype, name, itemsize=1):
+        def sbuf(columns, dtype, name, itemsize=1):
             if name not in offset_of:
                 return keep.tile([P, columns], dtype, name=name, align_bytes=64)[:]
             wide = span_of.get(name, 0) // itemsize
             whole = shared.tile([P, max(columns, wide)], dtype, name=name, align_bytes=64, offset=offset_of[name])
             return whole[:, 0:columns]
 
-        idx = keep.tile([P, S // 16], U16, name="idx")
-        idx2 = keep.tile([P, S2 // 16], U16, name="idx2")
-        tab_s = held(T, U8, "tab_s")
-        wb_s1 = held(K, U8, "wb_s1")
-        v_s1 = held(S, U8, "v_s1")
-        warm = held(2, F32, "warm", 4)
-        nc.vector.memset(tab_s.bitcast(I32), 0)
-        nc.vector.memset(warm[:, 0:1], 1.0)
-        nc.vector.memset(v_s1.bitcast(I32), 0)
+        idx = keep.tile([P, S // LIST_ROWS], U16, name="idx")
+        idx2 = keep.tile([P, S2 // LIST_ROWS], U16, name="idx2")
+
+        tab_s = sbuf(T, U8, "tab_s")
+        wb_s1 = sbuf(K, U8, "wb_s1")
+        v_s1 = sbuf(S, U8, "v_s1")
+        wb_s_raw = sbuf(K, U8, "wb_s_raw")
+        one = sbuf(1, F32, "one", 4)
+        unit = sbuf(2, F32, "unit")
+        for scale_tile in (tab_s, wb_s_raw, v_s1):
+            nc.gpsimd.memset(scale_tile.bitcast(I32), 0)
         nc.vector.memset(wb_s1.bitcast(I32), 0)
+        nc.gpsimd.memset(one, 1.0)
+        nc.gpsimd.tensor_copy(unit[:, 0:1], one)
 
         tab_w = {}
 
         def load_tab(a):
-            tab_w[a] = held(T, I32, f"tab_w{a}")
+            tab_w[a] = sbuf(T, I32, f"tab_w{a}")
             nc.sync.dma_start(tab_w[a], tab_words[a].rearrange("p t i -> p (t i)").bitcast(I32))
 
         wa_raw = {}
@@ -81,65 +100,81 @@ def tile_list_bond_strength_screen_kernel(tc, tab_words, tab_scales, offs, offs2
         def load_wa(a, b, pieces):
             width = PASS // pieces
             for piece in range(pieces):
-                raw = held(4 * width, F32, f"wa_raw{a}{b}_{piece}").rearrange("p (j c) -> p j c", j=4)
+                raw = sbuf(4 * width, F32, f"wa_raw{a}{b}_{piece}").rearrange("p (i c) -> p i c", i=4)
                 c0 = PASS * b + width * piece
-                nc.sync.dma_start(raw, wa[PASS * a : PASS * (a + 1), c0 : c0 + width].rearrange("(p j) c -> p j c", j=4))
+                nc.sync.dma_start(raw, wa[PASS * a : PASS * (a + 1), c0 : c0 + width].rearrange("(p i) c -> p i c", i=4))
                 wa_raw[(a, b, piece)] = raw
 
-        wb_w = {}
+        def load_scale_rows(scale_tile, scales):
+            for q in range(4):
+                nc.scalar.dma_start(scale_tile[32 * q : 32 * q + 8, :].bitcast(I32), scales[:, 4 * q : 4 * q + 4, :].bitcast(I32))
+
         v_w = {}
         v2_s = {}
-
-        def gather_v2_scales(part):
-            v2_s[part] = held(512, U8, f"v2_s{part}")
-            nc.vector.tensor_copy(v2_s[part], tab_s.indirect(idx2[:, 32 * part : 32 * (part + 1)]))
+        v2_w = {}
 
         def gather_v_words(a):
-            v_w[a] = held(S, U32, f"v_w{a}")
+            v_w[a] = sbuf(S, U32, f"v_w{a}")
             nc.vector.tensor_copy(v_w[a], tab_w[a].bitcast(U32).indirect(idx[:]))
+
+        def gather_v2_scales(part):
+            v2_s[part] = sbuf(PASS, U8, f"v2_s{part}")
+            columns = PASS // LIST_ROWS
+            nc.vector.tensor_copy(v2_s[part], tab_s.indirect(idx2[:, columns * part : columns * (part + 1)]))
+
+        def gather_v2_words(m0, count):
+            for b in range(2):
+                words = sbuf(count, U32, f"v2_w{b}_{m0}")
+                entries = idx2[:, m0 // LIST_ROWS : (m0 + count) // LIST_ROWS]
+                nc.vector.tensor_copy(words, tab_w[b].bitcast(U32).indirect(entries))
+                for m in range(m0, m0 + count, P):
+                    v2_w[(b, m)] = words[:, m - m0 : m - m0 + P]
 
         nc.sync.dma_start(idx[:], offs)
         nc.sync.dma_start(idx2[:], offs2)
-        wb_w_raw = held(4 * K, U8, "wb_w_raw")
+        wb_w_raw = sbuf(4 * K, U8, "wb_w_raw")
         nc.sync.dma_start(wb_w_raw.bitcast(I32).rearrange("p (a n) -> p a n", a=2), wb_words.bitcast(I32).rearrange("a p n -> p a n"))
+        load_scale_rows(tab_s, tab_scales)
         load_tab(0)
-        for q in range(4):
-            nc.scalar.dma_start(tab_s[32 * q : 32 * q + 8, :].bitcast(I32), tab_scales[:, 4 * q : 4 * q + 4, :].bitcast(I32))
-        nc.scalar.activation(warm[:, 1:2], warm[:, 0:1], ACT.Sqrt)
-        wb_s_raw = held(K, U8, "wb_s_raw")
-        nc.gpsimd.memset(wb_s_raw.bitcast(I32), 0)
-        for q in range(4):
-            nc.scalar.dma_start(wb_s_raw[32 * q : 32 * q + 8, :].bitcast(I32), wb_scales[:, 4 * q : 4 * q + 4, :].bitcast(I32))
+        load_scale_rows(wb_s_raw, wb_scales)
+
+        nc.scalar.activation(unit[:, 1:2], unit[:, 0:1], ACT.Sqrt)
+
+        wb_w = {}
         for b in range(2):
-            wb_w[b] = held(4 * PASS, U8, f"wb_w{b}")
-            src = wb_w_raw.bitcast(U16).rearrange("p (a b m t) -> p b a t m", a=2, b=2, t=4)
-            nc.vector.tensor_copy(wb_w[b].bitcast(U16).rearrange("p (a t m) -> p a t m", a=2, t=4), src[:, b])
+            wb_w[b] = sbuf(4 * PASS, U8, f"wb_w{b}")
+            words = wb_w_raw.bitcast(U16).rearrange("p (a b n t) -> p b a t n", a=2, b=2, t=4)
+            nc.vector.tensor_copy(wb_w[b].bitcast(U16).rearrange("p (a t n) -> p a t n", a=2, t=4), words[:, b])
         load_wa(0, 0, 1)
-        gain_sb = held(8, F32, "gain_sb").rearrange("p (b t) -> p b t", b=2)
-        nc.sync.dma_start(gain_sb, gain.rearrange("(b p t) -> p b t", b=2, t=4))
         load_tab(1)
-        load_wa(1, 0, 1)
+        gain_sb = sbuf(8, F32, "gain_sb").rearrange("p (b t) -> p b t", b=2)
+        nc.sync.dma_start(gain_sb, gain.rearrange("(b p t) -> p b t", b=2, t=4))
+
         gather_v_words(0)
-        v_s = held(S, U8, "v_s")
+        v_s = sbuf(S, U8, "v_s")
         nc.vector.tensor_copy(v_s, tab_s.indirect(idx[:]))
-        nc.scalar.dma_start(v_s1[0:100, :].bitcast(I32), v_s[4:104, :].bitcast(I32))
-        wb_s = held(K, U8, "wb_s")
-        nc.vector.tensor_copy(wb_s.rearrange("p (b t m) -> p b t m", b=2, t=4), wb_s_raw.rearrange("p (b m t) -> p b t m", b=2, t=4))
-        nc.scalar.dma_start(wb_s1[0:100, :].bitcast(I32), wb_s[4:104, :].bitcast(I32))
+        nc.scalar.dma_start(v_s1[0:SHIFT_ROWS, :].bitcast(I32), v_s[4 : 4 + SHIFT_ROWS, :].bitcast(I32))
+        wb_s = sbuf(K, U8, "wb_s")
+        nc.vector.tensor_copy(wb_s.rearrange("p (b t n) -> p b t n", b=2, t=4), wb_s_raw.rearrange("p (b n t) -> p b t n", b=2, t=4))
+        nc.sync.dma_start(wb_s1[0:SHIFT_ROWS, :].bitcast(I32), wb_s[4 : 4 + SHIFT_ROWS, :].bitcast(I32))
+        load_wa(1, 0, 1)
         load_wa(0, 1, 1)
         load_wa(1, 1, 2)
         gather_v2_scales(0)
+        gather_v2_scales(1)
         gather_v_words(1)
 
         b_sb = {}
 
         def product_b(b):
-            b_sb[b] = held(4 * S, F32, f"b_sb{b}").rearrange("p (t j) -> p t j", t=4)
+            b_sb[b] = sbuf(4 * S, F32, f"b_sb{b}").rearrange("p (t j) -> p t j", t=4)
             for t in range(4):
                 acc = psum.tile([P, S], F32, name="acc_b", tag=f"bank{t}")
                 for a in range(2):
-                    col = PASS * a + P * t
-                    nc.tensor.matmul_mx(acc[:], lhsT=wb_w[b][:, 2 * col : 2 * col + 2 * P].bitcast(FP4X4), lhsT_scale=(wb_s, wb_s1)[a][:, PASS * b + P * t : PASS * b + P * (t + 1)],
+                    word0 = PASS * a + P * t
+                    scale0 = PASS * b + P * t
+                    nc.tensor.matmul_mx(acc[:], lhsT=wb_w[b][:, 2 * word0 : 2 * (word0 + P)].bitcast(FP4X4),
+                                        lhsT_scale=(wb_s, wb_s1)[a][:, scale0 : scale0 + P],
                                         rhs=v_w[a].bitcast(FP8X4), rhs_scale=(v_s, v_s1)[a], start=(a == 0), stop=(a == 1))
                 nc.scalar.activation(b_sb[b][:, t, :], acc[:], ACT.Copy, scale=gain_sb[:, b, t : t + 1])
 
@@ -148,116 +183,110 @@ def tile_list_bond_strength_screen_kernel(tc, tab_words, tab_scales, offs, offs2
         wa_s = {}
 
         def round_wa(a, b, copies):
-            wa_bf[(a, b)] = held(4 * PASS, BF16, f"wa_bf{a}{b}", 2)
-            dst = wa_bf[(a, b)].rearrange("p (t m j) -> p m j t", t=4, j=4)
+            wa_bf[(a, b)] = sbuf(4 * PASS, BF16, f"wa_bf{a}{b}", 2)
+            rounded = wa_bf[(a, b)].rearrange("p (t n i) -> p n i t", t=4, i=4)
             share = P // len(copies)
-            for n, copy in enumerate(copies):
-                piece, m0 = (n, 0) if (a, b, n) in wa_raw and (a, b, 1) in wa_raw else (0, share * n)
-                copy(dst[:, share * n : share * (n + 1)], wa_raw[(a, b, piece)].rearrange("p j (m t) -> p m j t", t=4)[:, m0 : m0 + share])
+            for turn, copy in enumerate(copies):
+                piece, n0 = (turn, 0) if (a, b, 1) in wa_raw else (0, share * turn)
+                raw = wa_raw[(a, b, piece)].rearrange("p i (n t) -> p n i t", t=4)
+                copy(rounded[:, share * turn : share * (turn + 1)], raw[:, n0 : n0 + share])
 
         def quantize_wa(a, b):
-            wa_w[(a, b)] = held(PASS, U32, f"wa_w{a}{b}")
-            wa_s[(a, b)] = held(PASS, U8, f"wa_s{a}{b}")
+            wa_w[(a, b)] = sbuf(PASS, U32, f"wa_w{a}{b}")
+            wa_s[(a, b)] = sbuf(PASS, U8, f"wa_s{a}{b}")
             nc.vector.quantize_mx(wa_w[(a, b)].bitcast(FP8X4), wa_s[(a, b)], wa_bf[(a, b)])
-
-        h_w = {}
-        h_s = {}
 
         a_acc = {}
 
-        def product_a(b, half, first_bank):
+        def product_a(b, half):
             for quarter in range(2):
                 j0 = HALF * half + P * quarter
-                acc = psum.tile([P, 4, P], F32, name="acc_a", tag=f"bank{first_bank + quarter}")
+                acc = psum.tile([P, 4, P], F32, name="acc_a", tag=f"bank{A_BANKS[(b, half)] + quarter}")
                 a_acc[(b, half, quarter)] = acc
-                for step, a in enumerate((b, 1 - b)):
+                for a in range(2):
                     for t in range(4):
                         nc.tensor.matmul_mx(acc[:, t, :], lhsT=wa_w[(a, b)][:, P * t : P * (t + 1)].bitcast(FP8X4),
                                             lhsT_scale=wa_s[(a, b)][:, P * t : P * (t + 1)],
                                             rhs=v_w[a][:, j0 : j0 + P].bitcast(FP8X4), rhs_scale=v_s[4 * a :, j0 : j0 + P],
-                                            start=(step == 0 and t == 0), stop=(step == 1 and t == 3))
+                                            start=(a == 0 and t == 0), stop=(a == 1 and t == 3))
+
+        h_w = {}
+        h_s = {}
 
         def make_h(b, half):
-            h_bf = held(4 * HALF, BF16, f"h_bf{b}{half}", 2)
+            h_bf = sbuf(4 * HALF, BF16, f"h_bf{b}{half}", 2)
             for quarter in range(2):
                 j0 = HALF * half + P * quarter
-                acc = a_acc[(b, half, quarter)]
-                nc.vector.tensor_tensor(h_bf[:, 4 * P * quarter : 4 * P * (quarter + 1)].rearrange("p (c i t) -> p c t i", i=2, t=4),
-                                        acc[:].rearrange("p t (c i) -> p c t i", i=2),
-                                        b_sb[b][:, :, j0 : j0 + P].rearrange("p t (c i) -> p c t i", i=2), ALU.mult)
-            h_w[(b, half)] = held(HALF, U32, f"h_w{b}{half}")
-            h_s[(b, half)] = held(HALF, U8, f"h_s{b}{half}")
+                rounded = h_bf[:, 4 * P * quarter : 4 * P * (quarter + 1)]
+                nc.vector.tensor_tensor(rounded.rearrange("p (c u t) -> p c t u", u=2, t=4),
+                                        a_acc[(b, half, quarter)][:].rearrange("p t (c u) -> p c t u", u=2),
+                                        b_sb[b][:, :, j0 : j0 + P].rearrange("p t (c u) -> p c t u", u=2), ALU.mult)
+            h_w[(b, half)] = sbuf(HALF, U32, f"h_w{b}{half}")
+            h_s[(b, half)] = sbuf(HALF, U8, f"h_s{b}{half}")
             nc.vector.quantize_mx(h_w[(b, half)].bitcast(FP8X4), h_s[(b, half)], h_bf)
-
-        v2_w = {}
-
-        def gather_v2_words(m0, count):
-            for b in range(2):
-                words = held(count, U32, f"v2_w{b}{len(v2_w) // 2}")
-                nc.vector.tensor_copy(words, tab_w[b].bitcast(U32).indirect(idx2[:, m0 // 16 : (m0 + count) // 16]))
-                v2_w[(b, m0)] = words
 
         roots = []
 
-        def score(half, pair):
-            acc = psum.tile([P, 2, HALF], F32, name="acc_e", tag=f"bank{SCORE_BANKS[len(roots) % 4]}")
+        def square_on_scalar(squared, acc):
+            nc.scalar.activation(squared[:], acc[:], ACT.Square)
+
+        def square_on_vector(squared, acc):
+            copied = ring.tile([P, 2, HALF], F32, name="copied")
+            nc.vector.tensor_copy(copied[:], acc[:])
+            nc.vector.tensor_tensor(squared[:], acc[:], copied[:], ALU.mult)
+
+        def score(half, pair, square):
+            acc = psum.tile([P, 2, HALF], F32, name="acc_e", tag=f"bank{E_BANKS[len(roots) % len(E_BANKS)]}")
             for b in range(2):
-                for i in range(2):
-                    m0 = P * (2 * pair + i)
-                    part, c0 = divmod(m0, 512)
-                    first = max(start for pass_b, start in v2_w if start <= m0)
-                    nc.tensor.matmul_mx(acc[:, i, :], lhsT=v2_w[(b, first)][:, m0 - first : m0 - first + P].bitcast(FP8X4), lhsT_scale=v2_s[part][4 * b :, c0 : c0 + P],
-                                        rhs=h_w[(b, half)].bitcast(FP8X4), rhs_scale=h_s[(b, half)], start=(b == 0 and i == 0), stop=(b == 1 and i == 1))
-            sq = ring.tile([P, 2, HALF], F32, name="sq")
-            if len(roots) in (7,):
-                plain = ring.tile([P, 2, HALF], F32, name="plain", bufs=2)
-                nc.vector.tensor_copy(plain[:], acc[:])
-                nc.vector.tensor_tensor(sq[:], acc[:], plain[:], ALU.mult)
-            else:
-                nc.scalar.activation(sq[:], acc[:], ACT.Square)
+                for u in range(2):
+                    m0 = HALF * pair + P * u
+                    part, c0 = divmod(m0, PASS)
+                    nc.tensor.matmul_mx(acc[:, u, :], lhsT=v2_w[(b, m0)].bitcast(FP8X4), lhsT_scale=v2_s[part][4 * b :, c0 : c0 + P],
+                                        rhs=h_w[(b, half)].bitcast(FP8X4), rhs_scale=h_s[(b, half)],
+                                        start=(b == 0 and u == 0), stop=(b == 1 and u == 1))
+            squared = ring.tile([P, 2, HALF], F32, name="squared", bufs=5)
+            square(squared, acc)
             root = ring.tile([P, 2, HALF], F32, name="root", bufs=8)
-            nc.scalar.activation(root[:], sq[:], ACT.Sqrt, bias=1.0)
+            nc.scalar.activation(root[:], squared[:], ACT.Sqrt, bias=unit[:, 1:2])
             roots.append((half, pair, root))
 
         def finish(n):
             half, pair, root = roots[n]
-            res = held(2 * HALF, F32, f"res{n}").rearrange("p (i j) -> p i j", i=2)
-            for i in range(2):
-                nc.vector.tensor_scalar(res[:, i, :], root[:, i, :], level_sb[:, 2 * pair + i : 2 * pair + i + 1], None, ALU.subtract)
+            res = sbuf(2 * HALF, F32, f"res{n}").rearrange("p (u j) -> p u j", u=2)
+            for u in range(2):
+                nc.vector.tensor_scalar(res[:, u, :], root[:, u, :], level_sb[:, 2 * pair + u : 2 * pair + u + 1], None, ALU.subtract)
             rows = out[HALF * pair : HALF * (pair + 1), HALF * half : HALF * (half + 1)]
-            nc.sync.dma_start(rows.rearrange("(i p) j -> p i j", p=P), res)
+            nc.sync.dma_start(rows.rearrange("(u p) j -> p u j", p=P), res)
 
         round_wa(0, 0, [nc.scalar.copy])
         quantize_wa(0, 0)
-        gather_v2_words(0, 512)
-        gather_v2_scales(1)
+        gather_v2_words(0, 2 * HALF)
+        gather_v2_words(2 * HALF, HALF)
         product_b(0)
         round_wa(1, 0, [nc.scalar.copy])
         quantize_wa(1, 0)
-        level_sb = held(S2 // P, F32, "level_sb")
-        with nc.allow_non_contiguous_dma(reason="one level a partition"):
+        level_sb = sbuf(S2 // P, F32, "level_sb")
+        with nc.allow_non_contiguous_dma(reason="level[128 c + p] goes to partition p, column c"):
             nc.sync.dma_start(level_sb, level.rearrange("(c p) -> p c", p=P))
         round_wa(0, 1, [nc.vector.tensor_copy, nc.scalar.copy])
         product_b(1)
         round_wa(1, 1, [nc.vector.tensor_copy, nc.vector.tensor_copy])
-        quantize_wa(1, 1)
         quantize_wa(0, 1)
-        product_a(0, 0, 4)
-        product_a(0, 1, 6)
-        product_a(1, 0, 0)
+        quantize_wa(1, 1)
+        product_a(0, 0)
+        product_a(0, 1)
+        product_a(1, 0)
         make_h(0, 0)
-        product_a(1, 1, 4)
+        product_a(1, 1)
         make_h(1, 0)
         make_h(0, 1)
-        score(0, 0)
-        score(0, 1)
-        gather_v2_words(512, HALF)
-        score(0, 2)
+        for pair in range(3):
+            score(0, pair, square_on_scalar)
         make_h(1, 1)
         for pair in range(3):
-            score(1, pair)
-        gather_v2_words(768, HALF)
-        score(0, 3)
-        score(1, 3)
-        for n in range(8):
+            score(1, pair, square_on_scalar)
+        gather_v2_words(3 * HALF, HALF)
+        score(0, 3, square_on_scalar)
+        score(1, 3, square_on_vector)
+        for n in range(len(roots)):
             finish(n)

from contextlib import ExitStack

import concourse.mybir as mybir

F32 = mybir.dt.float32
BF16 = mybir.dt.bfloat16
I32 = mybir.dt.int32
U32 = mybir.dt.uint32
U16 = mybir.dt.uint16
U8 = mybir.dt.uint8
FP8X4 = mybir.dt.float8_e4m3fn_x4
FP4X4 = mybir.dt.float4_e2m1fn_x4
ACT = mybir.ActivationFunctionType
ALU = mybir.AluOpType

K, T, S, S2 = 1024, 2048, 512, 1024
P = 128
PASS = 512
HALF = 256
LIST_ROWS = 16
SHIFT_ROWS = 100
FLOPS = 2 * K * K * S * 2 + 2 * K * S2 * S

A_BANKS = {(0, 0): 4, (0, 1): 6, (1, 0): 0, (1, 1): 4}
E_BANKS = (2, 3, 0, 1)

HANDOVERS = [
    ("one", [("tab_w0", 8192)]),
    ("wb_s_raw", [("wa_raw10_0", 8192), ("wa_raw01_0", 8192), ("wa_raw11_0", 4096), ("wa_raw11_1", 4096),
                  ("v2_s0", 512), ("v2_s1", 512), ("wa_w00", 2048)]),
    ("wb_w_raw", [("wa_raw00_0", 8192), ("tab_w1", 8192), ("gain_sb", 64)]),
    ("wa_bf00", [("v2_w0_0", 2048), ("v2_w1_0", 2048), ("v2_w0_512", 1024), ("v2_w1_512", 1024)]),
    ("wb_w0", [("wa_bf10", 4096), ("wa_bf01", 4096)]),
    ("wa_bf11", [("h_bf00", 2048), ("h_bf01", 2048)]),
    ("h_bf10", [("h_bf11", 2048)]),
]
REGION_MIN = 4096
TAKEOVERS = [
    ("wa_w01", "wa_bf10", 64),
    ("wa_w11", "wa_bf01", 0),
    ("b_sb1", "wa_raw01_0", 0),
    ("level_sb", "wa_bf10", 0),
    ("v2_w0_768", "h_bf11", 0),
    ("v2_w1_768", "h_bf11", 1024),
    ("res0", "tab_w1", 0), ("res1", "tab_w1", 2048), ("res2", "tab_w1", 4096), ("res3", "tab_w1", 6144),
]


def tile_list_bond_strength_screen_kernel(tc, tab_words, tab_scales, offs, offs2, wa, wb_words, wb_scales, gain, level, out):
    nc = tc.nc
    offset_of = {}
    span_of = {}
    end = 0
    for earlier, later in HANDOVERS:
        offset_of[earlier] = end
        span_of[earlier] = sum(size for name, size in later)
        for name, size in later:
            offset_of[name] = end
            end = end + size
        end = max(end, offset_of[earlier] + REGION_MIN)
    for name, earlier, skip in TAKEOVERS:
        offset_of[name] = offset_of[earlier] + skip

    with ExitStack() as ctx:
        keep = ctx.enter_context(tc.tile_pool(name="keep", bufs=1))
        shared = ctx.enter_context(tc.tile_pool(name="shared", bufs=1))
        ring = ctx.enter_context(tc.tile_pool(name="ring", bufs=1))
        psum = ctx.enter_context(tc.psum_pool(name="psum", bufs=1))

        def sbuf(columns, dtype, name, itemsize=1):
            if name not in offset_of:
                return keep.tile([P, columns], dtype, name=name, align_bytes=64)[:]
            wide = span_of.get(name, 0) // itemsize
            whole = shared.tile([P, max(columns, wide)], dtype, name=name, align_bytes=64, offset=offset_of[name])
            return whole[:, 0:columns]

        idx = keep.tile([P, S // LIST_ROWS], U16, name="idx")
        idx2 = keep.tile([P, S2 // LIST_ROWS], U16, name="idx2")

        tab_s = sbuf(T, U8, "tab_s")
        wb_s1 = sbuf(K, U8, "wb_s1")
        v_s1 = sbuf(S, U8, "v_s1")
        wb_s_raw = sbuf(K, U8, "wb_s_raw")
        one = sbuf(1, F32, "one", 4)
        unit = sbuf(2, F32, "unit")
        for scale_tile in (tab_s, wb_s_raw, v_s1):
            nc.gpsimd.memset(scale_tile.bitcast(I32), 0)
        nc.vector.memset(wb_s1.bitcast(I32), 0)
        nc.gpsimd.memset(one, 1.0)
        nc.gpsimd.tensor_copy(unit[:, 0:1], one)

        tab_w = {}

        def load_tab(a):
            tab_w[a] = sbuf(T, I32, f"tab_w{a}")
            nc.sync.dma_start(tab_w[a], tab_words[a].rearrange("p t i -> p (t i)").bitcast(I32))

        wa_raw = {}

        def load_wa(a, b, pieces):
            width = PASS // pieces
            for piece in range(pieces):
                raw = sbuf(4 * width, F32, f"wa_raw{a}{b}_{piece}").rearrange("p (i c) -> p i c", i=4)
                c0 = PASS * b + width * piece
                nc.sync.dma_start(raw, wa[PASS * a : PASS * (a + 1), c0 : c0 + width].rearrange("(p i) c -> p i c", i=4))
                wa_raw[(a, b, piece)] = raw

        def load_scale_rows(scale_tile, scales):
            for q in range(4):
                nc.scalar.dma_start(scale_tile[32 * q : 32 * q + 8, :].bitcast(I32), scales[:, 4 * q : 4 * q + 4, :].bitcast(I32))

        v_w = {}
        v2_s = {}
        v2_w = {}

        def gather_v_words(a):
            v_w[a] = sbuf(S, U32, f"v_w{a}")
            nc.vector.tensor_copy(v_w[a], tab_w[a].bitcast(U32).indirect(idx[:]))

        def gather_v2_scales(part):
            v2_s[part] = sbuf(PASS, U8, f"v2_s{part}")
            columns = PASS // LIST_ROWS
            nc.vector.tensor_copy(v2_s[part], tab_s.indirect(idx2[:, columns * part : columns * (part + 1)]))

        def gather_v2_words(m0, count):
            for b in range(2):
                words = sbuf(count, U32, f"v2_w{b}_{m0}")
                entries = idx2[:, m0 // LIST_ROWS : (m0 + count) // LIST_ROWS]
                nc.vector.tensor_copy(words, tab_w[b].bitcast(U32).indirect(entries))
                for m in range(m0, m0 + count, P):
                    v2_w[(b, m)] = words[:, m - m0 : m - m0 + P]

        nc.sync.dma_start(idx[:], offs)
        nc.sync.dma_start(idx2[:], offs2)
        wb_w_raw = sbuf(4 * K, U8, "wb_w_raw")
        nc.sync.dma_start(wb_w_raw.bitcast(I32).rearrange("p (a n) -> p a n", a=2), wb_words.bitcast(I32).rearrange("a p n -> p a n"))
        load_scale_rows(tab_s, tab_scales)
        load_tab(0)
        load_scale_rows(wb_s_raw, wb_scales)

        nc.scalar.activation(unit[:, 1:2], unit[:, 0:1], ACT.Sqrt)

        wb_w = {}
        for b in range(2):
            wb_w[b] = sbuf(4 * PASS, U8, f"wb_w{b}")
            words = wb_w_raw.bitcast(U16).rearrange("p (a b n t) -> p b a t n", a=2, b=2, t=4)
            nc.vector.tensor_copy(wb_w[b].bitcast(U16).rearrange("p (a t n) -> p a t n", a=2, t=4), words[:, b])
        load_wa(0, 0, 1)
        load_tab(1)
        gain_sb = sbuf(8, F32, "gain_sb").rearrange("p (b t) -> p b t", b=2)
        nc.sync.dma_start(gain_sb, gain.rearrange("(b p t) -> p b t", b=2, t=4))

        gather_v_words(0)
        v_s = sbuf(S, U8, "v_s")
        nc.vector.tensor_copy(v_s, tab_s.indirect(idx[:]))
        nc.scalar.dma_start(v_s1[0:SHIFT_ROWS, :].bitcast(I32), v_s[4 : 4 + SHIFT_ROWS, :].bitcast(I32))
        wb_s = sbuf(K, U8, "wb_s")
        nc.vector.tensor_copy(wb_s.rearrange("p (b t n) -> p b t n", b=2, t=4), wb_s_raw.rearrange("p (b n t) -> p b t n", b=2, t=4))
        nc.sync.dma_start(wb_s1[0:SHIFT_ROWS, :].bitcast(I32), wb_s[4 : 4 + SHIFT_ROWS, :].bitcast(I32))
        load_wa(1, 0, 1)
        load_wa(0, 1, 1)
        load_wa(1, 1, 2)
        gather_v2_scales(0)
        gather_v2_scales(1)
        gather_v_words(1)

        b_sb = {}

        def product_b(b):
            b_sb[b] = sbuf(4 * S, F32, f"b_sb{b}").rearrange("p (t j) -> p t j", t=4)
            for t in range(4):
                acc = psum.tile([P, S], F32, name="acc_b", tag=f"bank{t}")
                for a in range(2):
                    word0 = PASS * a + P * t
                    scale0 = PASS * b + P * t
                    nc.tensor.matmul_mx(acc[:], lhsT=wb_w[b][:, 2 * word0 : 2 * (word0 + P)].bitcast(FP4X4),
                                        lhsT_scale=(wb_s, wb_s1)[a][:, scale0 : scale0 + P],
                                        rhs=v_w[a].bitcast(FP8X4), rhs_scale=(v_s, v_s1)[a], start=(a == 0), stop=(a == 1))
                nc.scalar.activation(b_sb[b][:, t, :], acc[:], ACT.Copy, scale=gain_sb[:, b, t : t + 1])

        wa_bf = {}
        wa_w = {}
        wa_s = {}

        def round_wa(a, b, copies):
            wa_bf[(a, b)] = sbuf(4 * PASS, BF16, f"wa_bf{a}{b}", 2)
            rounded = wa_bf[(a, b)].rearrange("p (t n i) -> p n i t", t=4, i=4)
            share = P // len(copies)
            for turn, copy in enumerate(copies):
                piece, n0 = (turn, 0) if (a, b, 1) in wa_raw else (0, share * turn)
                raw = wa_raw[(a, b, piece)].rearrange("p i (n t) -> p n i t", t=4)
                copy(rounded[:, share * turn : share * (turn + 1)], raw[:, n0 : n0 + share])

        def quantize_wa(a, b):
            wa_w[(a, b)] = sbuf(PASS, U32, f"wa_w{a}{b}")
            wa_s[(a, b)] = sbuf(PASS, U8, f"wa_s{a}{b}")
            nc.vector.quantize_mx(wa_w[(a, b)].bitcast(FP8X4), wa_s[(a, b)], wa_bf[(a, b)])

        a_acc = {}

        def product_a(b, half):
            for quarter in range(2):
                j0 = HALF * half + P * quarter
                acc = psum.tile([P, 4, P], F32, name="acc_a", tag=f"bank{A_BANKS[(b, half)] + quarter}")
                a_acc[(b, half, quarter)] = acc
                for a in range(2):
                    for t in range(4):
                        nc.tensor.matmul_mx(acc[:, t, :], lhsT=wa_w[(a, b)][:, P * t : P * (t + 1)].bitcast(FP8X4),
                                            lhsT_scale=wa_s[(a, b)][:, P * t : P * (t + 1)],
                                            rhs=v_w[a][:, j0 : j0 + P].bitcast(FP8X4), rhs_scale=v_s[4 * a :, j0 : j0 + P],
                                            start=(a == 0 and t == 0), stop=(a == 1 and t == 3))

        h_w = {}
        h_s = {}

        def make_h(b, half):
            h_bf = sbuf(4 * HALF, BF16, f"h_bf{b}{half}", 2)
            for quarter in range(2):
                j0 = HALF * half + P * quarter
                rounded = h_bf[:, 4 * P * quarter : 4 * P * (quarter + 1)]
                nc.vector.tensor_tensor(rounded.rearrange("p (c u t) -> p c t u", u=2, t=4),
                                        a_acc[(b, half, quarter)][:].rearrange("p t (c u) -> p c t u", u=2),
                                        b_sb[b][:, :, j0 : j0 + P].rearrange("p t (c u) -> p c t u", u=2), ALU.mult)
            h_w[(b, half)] = sbuf(HALF, U32, f"h_w{b}{half}")
            h_s[(b, half)] = sbuf(HALF, U8, f"h_s{b}{half}")
            nc.vector.quantize_mx(h_w[(b, half)].bitcast(FP8X4), h_s[(b, half)], h_bf)

        roots = []

        def square_on_scalar(squared, acc):
            nc.scalar.activation(squared[:], acc[:], ACT.Square)

        def square_on_vector(squared, acc):
            copied = ring.tile([P, 2, HALF], F32, name="copied")
            nc.vector.tensor_copy(copied[:], acc[:])
            nc.vector.tensor_tensor(squared[:], acc[:], copied[:], ALU.mult)

        def score(half, pair, square):
            acc = psum.tile([P, 2, HALF], F32, name="acc_e", tag=f"bank{E_BANKS[len(roots) % len(E_BANKS)]}")
            for b in range(2):
                for u in range(2):
                    m0 = HALF * pair + P * u
                    part, c0 = divmod(m0, PASS)
                    nc.tensor.matmul_mx(acc[:, u, :], lhsT=v2_w[(b, m0)].bitcast(FP8X4), lhsT_scale=v2_s[part][4 * b :, c0 : c0 + P],
                                        rhs=h_w[(b, half)].bitcast(FP8X4), rhs_scale=h_s[(b, half)],
                                        start=(b == 0 and u == 0), stop=(b == 1 and u == 1))
            squared = ring.tile([P, 2, HALF], F32, name="squared", bufs=5)
            square(squared, acc)
            root = ring.tile([P, 2, HALF], F32, name="root", bufs=8)
            nc.scalar.activation(root[:], squared[:], ACT.Sqrt, bias=unit[:, 1:2])
            roots.append((half, pair, root))

        def finish(n):
            half, pair, root = roots[n]
            res = sbuf(2 * HALF, F32, f"res{n}").rearrange("p (u j) -> p u j", u=2)
            for u in range(2):
                nc.vector.tensor_scalar(res[:, u, :], root[:, u, :], level_sb[:, 2 * pair + u : 2 * pair + u + 1], None, ALU.subtract)
            rows = out[HALF * pair : HALF * (pair + 1), HALF * half : HALF * (half + 1)]
            nc.sync.dma_start(rows.rearrange("(u p) j -> p u j", p=P), res)

        round_wa(0, 0, [nc.scalar.copy])
        quantize_wa(0, 0)
        gather_v2_words(0, 2 * HALF)
        gather_v2_words(2 * HALF, HALF)
        product_b(0)
        round_wa(1, 0, [nc.scalar.copy])
        quantize_wa(1, 0)
        level_sb = sbuf(S2 // P, F32, "level_sb")
        with nc.allow_non_contiguous_dma(reason="level[128 c + p] goes to partition p, column c"):
            nc.sync.dma_start(level_sb, level.rearrange("(c p) -> p c", p=P))
        round_wa(0, 1, [nc.vector.tensor_copy, nc.scalar.copy])
        product_b(1)
        round_wa(1, 1, [nc.vector.tensor_copy, nc.vector.tensor_copy])
        quantize_wa(0, 1)
        quantize_wa(1, 1)
        product_a(0, 0)
        product_a(0, 1)
        product_a(1, 0)
        make_h(0, 0)
        product_a(1, 1)
        make_h(1, 0)
        make_h(0, 1)
        for pair in range(3):
            score(0, pair, square_on_scalar)
        make_h(1, 1)
        for pair in range(3):
            score(1, pair, square_on_scalar)
        gather_v2_words(3 * HALF, HALF)
        score(0, 3, square_on_scalar)
        score(1, 3, square_on_vector)
        for n in range(len(roots)):
            finish(n)
